import numpy as np, ml_dtypes
CORES = [3,7,11,15,131,135,139,143]
N = 8
import mx_ref
BF = ml_dtypes.bfloat16
def gentries(a):
    return np.ascontiguousarray(a.reshape(8, 16, -1).transpose(0, 2, 1)).reshape(8, -1)
def gtable(e):
    e = np.asarray(e); return np.ascontiguousarray(e.reshape(8, -1, 16).transpose(0, 2, 1)).reshape(128, -1).astype(np.int32)
def gcols(t, e):
    v = np.concatenate([t.reshape(8, 16, -1, 4), np.zeros((8, 16, 1, 4), BF)], axis=2)
    return np.ascontiguousarray(np.stack([v[g][:, e[g]] for g in range(8)])).reshape(128, -1)
def tile(rs):
    return np.stack(rs, axis=2).reshape(128, -1).astype(BF)
def cut(t, i, w=512):
    return t[:, w * i:w * i + w]
def pick(q, e):
    c = np.concatenate([q[0].reshape(128, -1, 4), np.zeros((128, 1, 4), np.uint8)], axis=1); s = np.concatenate([q[1], np.ones((16, 1), np.uint8)], axis=1)
    return (np.ascontiguousarray(c[:, e].reshape(128, -1)), np.ascontiguousarray(s[:, e]))
def join(*qs):
    return (np.concatenate([q[0] for q in qs], axis=1), np.concatenate([q[1] for q in qs], axis=1))
def put(q, e, v):
    c, s = q[0].reshape(128, -1, 4).copy(), q[1].copy(); c[:, e] = v[0].reshape(128, -1, 4); s[:, e] = v[1]
    return (c.reshape(128, -1), s)
def pk(c, s):
    return (np.ascontiguousarray(c), mx_ref.live(s))
def emit(q):
    return q[0], q[1]
def packed(v, rng):
    q = [mx_ref.quantize(np.ascontiguousarray(v[r])) for r in range(N)]
    return np.stack([a for a, b in q]), np.stack([mx_ref.plane(b, rng) for a, b in q])
def values_of_codes():
    e, c = np.zeros((128, 128, 4), np.float32), np.zeros((128, 2, 4), np.uint8)
    e[np.arange(128), np.arange(128), 0] = 1
    c[:127, :, 0] = np.arange(256).reshape(2, 128).T[:127]
    return mx_ref.matmul(mx_ref.quantize(e.reshape(128, 512).astype(BF)), (c.reshape(128, 8), np.full((16, 2), 127, np.uint8))).T.reshape(-1).astype(np.float64)
CODE_VALUE, SCALE_VALUE = values_of_codes(), 2.0 ** (np.arange(256) - 127.0)
def decode(q):
    return (CODE_VALUE[q[0]].reshape(16, 8, -1, 4) * SCALE_VALUE[q[1]][:, None, :, None] + 0.0).reshape(128, -1).astype(np.float32)
def f(rng, *shape):
    return mx_ref.flush((rng.standard_normal(shape, dtype=np.float32) * np.exp2(rng.integers(-2, 3, shape[:-1] + (1,)))).astype(BF))
def wide(rng, *shape, cols=0):
    v = rng.standard_normal(shape, dtype=np.float32) * np.exp2(rng.integers(-12, 13, shape)).astype(np.float32)
    if cols: v *= np.repeat(np.exp2(rng.integers(-cols, cols + 1, shape[:-2] + (1, shape[-1] // 4))) * (rng.random(shape[:-2] + (1, shape[-1] // 4)) > 0.0625), 4, axis=-1).astype(np.float32)
    return mx_ref.flush(v.astype(BF))
C, A, R = 448, 192, 3
STEP = [1, 2, 4]
def partner(r, t):
    return r ^ STEP[t]
def big(v, k):
    v = v.astype(np.float32) * np.float32(k)
    v[np.abs(v) < np.float32(2.0 ** -16)] = 0
    return v.astype(BF)
def common(w, rng):
    c, p = packed(np.stack([w] * N), rng)
    return {"wc": c, "ws": p}
def weights(rng, q=-1):
    w = big(f(rng, 128, 2048), 1).reshape(128, 4, 128, 4)
    if q >= 0:
        w[16 * q:16 * q + 8] = 0
        for i in range(16 * q, 16 * q + 8):
            w[:, :, i] = 0
            for b in range(4): w[i, b, i, b] = 64
    return common(w.reshape(128, 2048), rng)
def numbers_of(rng):
    return {"x": big(f(rng, N, 128, 4 * C), 1), "u": np.array(f(rng, N, 128, 512)), "v": np.array(f(rng, N, 128, 512))}
def lists_of(rng):
    return {"m": np.argsort(rng.random((N, 8, C)), axis=2), "la": rng.integers(0, C, (N, 8, R * A)), "lb": rng.integers(0, C, (N, 8, R * A)),
            "ld": np.argsort(rng.random((N, 8, R, C)), axis=3)[:, :, :, :A].reshape(N, 8, R * A)}
def stored(l):
    return {k: np.stack([gtable(e) for e in l[k]]) for k in ("m", "la", "lb", "ld")}
def setup_inputs(rng):
    return {**numbers_of(rng), **stored(lists_of(rng)), **weights(rng)}
def setup_inputs_rolls(rng):
    d, l = numbers_of(rng), lists_of(rng)
    q = int(rng.integers(8))
    o = rng.permutation(N)
    back = []
    for r in range(N):
        g = rng.permutation(8)
        if o[r] % 3 == 2: g = rng.permutation(7)
        while abs(int(g[0]) - int(g[1])) < 2: g = np.roll(g, 1)
        back.append([[(0, 1), (1, 2), (2, 3)], [(0, 1), (2, 3), (0, 2)], [(0, 1), (0, 1), (0, 1)]][o[r] % 3])
        back[r] = [[int(g[i]) for i in e] for e in back[r]]
    size = np.exp2(np.array([-30.0, -12.0, 0.0, 10.0])[rng.permutation(N) % 4]).astype(np.float32)
    mark = np.zeros((27, 8, 4), np.float32)
    for k in range(9):
        for i in range(2):
            mark[k + 9 * i, :, 0] = i
            if k < 8: mark[k + 9 * i, k] = (0, 2, 0, 0)
        mark[18 + k, :, 1] = 2
        if k < 8: mark[18 + k, k] = 0
    x = d["x"].reshape(N, 8, 16, C, 4)
    u = d["u"].reshape(N, 128, 128, 4)
    u[:, :, ::16] = 0
    one = np.ones(N, np.float32)
    for r in range(N):
        if size[r] < 2.0 ** -20:
            for t in range(R): one[partner(r, t)] = 2.0 ** -30
    for g in range(8):
        u[:, 16 * q + g, 16 * g, 0] = one.astype(BF)
        u[:, 16 * q + g, 16 * g, 1] = (-one).astype(BF)
    for r in range(N):
        e = rng.permutation(C)
        written, pool = e[:A], e[A:]
        kind = rng.integers(0, 27, C)
        kind[l["m"][r, q, pool]] = np.arange(C - A) % 27
        x[r, q, :8] = (mark[kind].transpose(1, 0, 2) * size[r]).astype(BF)
        for t in range(R):
            l["ld"][r, q, A * t:A * t + A] = rng.permutation(written)
            p = back[partner(r, t)][t]
            most = o[partner(r, t)] == 2 and t == R - 1
            h = A - 1 if most else int(rng.integers(2, A // 4))
            n = np.full(8, h - 1)
            if (o[partner(r, t)] + t) % 2 == 0:
                n[min(p):] = h
                n[max(p)] = h + 1
            else:
                n[p] = h
                n[max(p) + 1:] = h
            k = np.full(2 * A, 8)
            if most: k[:A] = 26
            s = np.repeat(18 + np.arange(8), A - n) if most else np.repeat(np.arange(8), n)
            k[:len(s)] = s
            e = pool[k + 9 * rng.integers(0, 2, 2 * A) * (k < 9) + 27 * rng.integers(0, (C - A) // 27, 2 * A)]
            j = rng.permutation(A)
            l["la"][r, q, A * t:A * t + A] = e[:A][j]
            l["lb"][r, q, A * t:A * t + A] = e[A:][j]
    return {"x": x.reshape(N, 128, 4 * C), "u": u.reshape(N, 128, 512), "v": d["v"], **stored(l), **weights(rng, q)}
def setup_inputs_lists(rng):
    d, l = numbers_of(rng), lists_of(rng)
    o = rng.permutation(N)
    for r in range(N):
        if o[r] == 2:
            l["m"][r] = rng.permutation(C)[None, :]
            e = l["m"][r, 0, C - 8:]
            x = np.zeros((128, C, 4), BF)
            x[:, e] = d["x"][r].reshape(128, C, 4)[:, e]
            d["x"][r] = x.reshape(128, 4 * C)
            l["la"][r] %= C - 8
            l["lb"][r] %= C - 8
            l["ld"][r] = np.argsort(rng.random((8, R, C - 8)), axis=2)[:, :, :A].reshape(8, R * A)
        elif o[r] % 2:
            e = np.repeat(l["ld"][r, :, :1], R * A, axis=1)
            l["la"][r] = e
            l["lb"][r] = e
        else:
            e = l["ld"][r, :, :A].copy()
            l["ld"][r] = np.tile(e, (1, R))
            l["la"][r] = np.tile(e, (1, R))
            l["lb"][r] = np.tile(e[:, ::-1], (1, R))
    return {**d, **stored(l), **weights(rng)}
def setup_inputs_huge(rng):
    d, l = numbers_of(rng), lists_of(rng)
    o = rng.permutation(N)
    g = np.ones((N, 8))
    for r in range(N):
        if o[r] == 0: g[r] = -1
        if o[r] == 2: g[r, 0] = -1
        if o[r] > 2: g[r] = rng.permutation(8) % 2 * 2.0 - 1.0
    x = 2.0 ** 28 * (1.5 + 0.5 * rng.random((N, 128, 4 * C)))
    u = d["u"].reshape(N, 128, 128, 4)
    u[:, :, ::16] = (2.0 ** 30 * (0.75 + 0.25 * rng.random((N, 128, 8, 4))) * g[:, None, :, None]).astype(np.float32).astype(BF)
    w = np.zeros((128, 4, 128, 4), np.float32)
    i = np.arange(128)
    for b in range(4): w[i, b, i, b] = 32
    return {"x": x.astype(np.float32).astype(BF), "u": u.reshape(N, 128, 512), "v": d["v"], **stored(l), **common(w.reshape(128, 2048).astype(BF), rng)}
def setup_inputs_spread(rng):
    d = setup_inputs(rng)
    d["x"] = big(wide(rng, N, 128, 4 * C, cols=6), 1)
    return d
def check_inputs(d):
    b = []
    for k in ("x", "u", "v"):
        a = np.abs(d[k].astype(np.float32))
        if not (np.isfinite(a).all() and ((a == 0) | (a >= 2.0 ** -30) & (a <= 2.0 ** 30)).all()): b.append("a value of " + k)
    for r in range(N):
        if (np.sort(gentries(d["m"][r]), axis=1) != np.arange(C)).any(): b.append("m: a group's entries aren't a permutation")
        for k in ("la", "lb", "ld"):
            if ((d[k][r] < 0) | (d[k][r] >= C)).any(): b.append("an entry of " + k)
        s = np.sort(gentries(d["ld"][r]).reshape(8, R, A), axis=2)
        if (s[:, :, 1:] == s[:, :, :-1]).any(): b.append("ld: equal entries of a group in a round")
    if (d["wc"] != d["wc"][:1]).any(): b.append("wc differs between ranks")
    s = [mx_ref.live(p) for p in d["ws"]]
    if any((p != s[0]).any() for p in s): b.append("ws differs between ranks")
    return b
def reference(x, u, v, m, la, lb, ld, wc, ws):
    w = pk(wc[0], ws[0])
    qu = [mx_ref.quantize(u[r]) for r in range(N)]
    kept = [x[r] for r in range(N)]
    maps = [[gentries(m[r]).astype(np.int64)] for r in range(N)]
    for t in range(R):
        sent = []
        for r in range(N):
            now = maps[r][t]
            one = gcols(kept[r], np.take_along_axis(now, gentries(la[r])[:, A * t:A * t + A], axis=1))
            two = gcols(kept[r], np.take_along_axis(now, gentries(lb[r])[:, A * t:A * t + A], axis=1))
            q = mx_ref.quantize((one.astype(np.float32) + two.astype(np.float32)).astype(BF))
            h = tile([np.maximum(mx_ref.matmul(pick(w, np.arange(128 * b, 128 * b + 128)), q), np.float32(0.0)) * np.float32(0.015625) for b in range(4)])
            sent.append(mx_ref.quantize(h))
        came = decode(join(*sent)).astype(BF)
        for r in range(N):
            e = partner(r, t)
            yes = mx_ref.matmul(qu[r], sent[e])[::16] + np.float32(0.0) >= 0
            kept[r] = np.concatenate([kept[r], cut(came, e, 4 * A)], axis=1)
            to = gentries(ld[r])[:, A * t:A * t + A]
            new = maps[r][t].copy()
            for g in range(8): new[g, to[g][yes[g]]] = C + A * t + np.flatnonzero(yes[g])
            n = np.sum(~yes, axis=1)
            for g in np.argsort(-n, kind="stable")[:2]: new[g] = maps[r][max(t - 1, 0)][g]
            maps[r].append(new)
    y, om = np.zeros((N, 128, C), np.float32), np.zeros((N, 8, C), np.float32)
    oc, osc = np.zeros((N, 128, 4 * C), np.uint8), np.zeros((N, 16, C), np.uint8)
    for r in range(N):
        q = mx_ref.quantize(gcols(kept[r], maps[r][R]))
        y[r] = mx_ref.matmul(mx_ref.quantize(v[r]), q)
        om[r] = maps[r][R]
        oc[r], osc[r] = emit(q)
    return {"y": y, "om": om, "oc": oc, "osc": osc}

@@ -1,0 +1,411 @@
+from concourse.mybir import dt, AluOpType as Op, ActivationFunctionType as Fn
+
+C, A, ROUNDS = 448, 192, 3
+NA = 96
+NB = A - NA
+MINC = 128
+WB = max(MINC, NB)
+RAMP, DROP = 2048.0, 65536.0
+TINY = 2.0 ** -126
+HALF = C / 2
+ZCUT = [0, 8, 24, 48]
+TCUT = [0, 256, 448]
+TSHARE = [36, 20]
+LAND = MINC + ROUNDS * A
+F32, BF, I32, U16, Q4, U8 = "float32", "bfloat16", "int32", "uint16", "float8_e4m3fn_x4", "uint8"
+LM, LD, LA, LB, LI, LS, LE = 0, 28, 64, 100, 136, 164, 172
+
+SCRATCH = {
+    "lst": ("sbuf", [128, LI], I32), "lu": ("sbuf", [128, LI], U16), "ids": ("sbuf", [128, LE - LI], F32),
+    "lf": ("sbuf", [128, LE], F32), "lsh": ("sbuf", [128, LE], U16),
+    "fil": ("sbuf", [128, 4096], BF), "maps": ("sbuf", [128, 5 * C], F32),
+    "cnt": ("sbuf", [128, ROUNDS * A], F32), "pcol": ("sbuf", [128, 1], I32), "k4": ("sbuf", [128, 4], F32),
+    "c16": ("sbuf", [128, 28], F32), "ci": ("sbuf", [128, 8], I32), "cf": ("sbuf", [128, 8], F32),
+    "c4": ("sbuf", [128, 8], F32), "addc": ("sbuf", [128, 2], F32), "tiny": ("sbuf", [128, 1], F32),
+    "cpat": ("sbuf", [128, C], F32), "c32": ("sbuf", [128, 32], F32), "upick": ("sbuf", [128, 16], U16),
+    "tie": ("sbuf", [128, 36], F32),
+    "zero": ("sbuf", [128, 512], BF), "ones": ("sbuf", [128, 1032], BF), "unit": ("sbuf", [128, 1032], BF),
+    "qe": ("sbuf", [128, 512], Q4), "se": ("sbuf", [128, 512], U8),
+    "qw": ("sbuf", [128, 512], Q4), "sw": ("sbuf", [128, 512], U8),
+    "ut": ("sbuf", [128, 512], BF), "vt": ("sbuf", [128, 512], BF),
+    "qu": ("sbuf", [128, 128], Q4), "su": ("sbuf", [128, 128], U8),
+    "qp": ("sbuf", [128, 256], Q4), "sp": ("sbuf", [128, 256], U8),
+    "qv": ("sbuf", [128, 128], Q4), "sv": ("sbuf", [128, 128], U8),
+    "row": ("sbuf", [128, 2 * A], F32), "scn": ("sbuf", [128, 2 * A], F32), "off": ("sbuf", [128, 112], U16),
+    "opb": ("sbuf", [128, 4 * A], BF),
+    "za": ("sbuf", [128, 4 * MINC], BF), "zb": ("sbuf", [128, 4 * WB], BF),
+    "ha": ("sbuf", [128, 4 * MINC], BF), "hb": ("sbuf", [128, 4 * WB], BF),
+    "qza": ("sbuf", [128, ROUNDS * MINC], Q4), "sza": ("sbuf", [128, ROUNDS * MINC], U8),
+    "qhb": ("sbuf", [128, ROUNDS * WB], Q4), "shb": ("sbuf", [128, ROUNDS * WB], U8),
+    "qzb": ("sbuf", [128, WB], Q4), "szb": ("sbuf", [128, WB], U8),
+    "qga": ("sbuf", [128, MINC], Q4), "sga": ("sbuf", [128, MINC], U8),
+    "ql": ("sbuf", [128, LAND], Q4), "sl": ("sbuf", [128, LAND], U8),
+    "sgn": ("sbuf", [128, 2 * A], F32), "cand": ("sbuf", [128, ROUNDS * 2 * A], F32), "nv": ("sbuf", [128, 2 * A], F32),
+    "junk": ("sbuf", [128, A], BF), "acc": ("sbuf", [128, 8], F32), "key": ("sbuf", [128, 64], F32),
+    "cmp": ("sbuf", [128, 8], F32), "keep": ("sbuf", [128, 1], F32),
+    "sel": ("sbuf", [128, 2 * C], F32), "omr": ("sbuf", [128, C], F32),
+    "tt": ("sbuf", [128, 4 * C], BF), "qt": ("sbuf", [128, C], Q4), "st": ("sbuf", [128, C], U8),
+    "ysb": ("sbuf", [128, C], F32),
+    "ps": ("psum", [128, 4096], F32),
+}
+SEMAPHORES = (["nv_", "ns_", "nt_", "ng_", "sent"] + ["dma%d" % k for k in range(28)]
+              + ["arr%d" % k for k in range(2 * ROUNDS)])
+
+
+def rank_program(g, core, T, topo):
+    rank = T.rank_of(core)
+    if rank is None:
+        return
+    queue = {"v": g.vector, "s": g.scalar, "t": g.tensor, "g": g, "y": g.sync}
+    counter = {"v": "nv_", "s": "ns_", "t": "nt_", "g": "ng_"}
+    known = {q: {} for q in queue}
+    total, log, ndma = {}, {}, [0]
+
+    def at(name, a=0, b=None, step=1, rows=slice(None)):
+        b = SCRATCH[name][1][1] if b is None else b
+        if name == "ps":
+            return T.ps[:, a:b], (name, 1 << (a // 512))
+        bits = 0
+        for c in range(a, b, step):
+            bits |= 1 << c
+        return (T[name][rows, a:b:step] if step > 1 else T[name][rows, a:b]), (name, bits)
+
+    def order(q, reads, writes):
+        writes = list(writes) + [r for r in reads if r[0] == "ps"]
+        need = []
+        for regs, w in ((reads, False), (writes, True)):
+            for name, bits in regs:
+                need += [e for b, e, ew in log.get(name, []) if b & bits and (w or ew)]
+        for sem, n, clock, seq in sorted(need, key=lambda e: -e[3]):
+            if known[q].get(sem, 0) < n:
+                queue[q].wait_ge(T.sem[sem], n)
+                for s, k in list(clock.items()) + [(sem, n)]:
+                    known[q][s] = max(known[q].get(s, 0), k)
+        return writes
+
+    def note(reads, writes, sem, inc, clock):
+        total[sem] = total.get(sem, 0) + inc
+        e = (sem, total[sem], dict(clock), sum(total.values()))
+        for regs, w in ((reads, False), (writes, True)):
+            for name, bits in regs:
+                log.setdefault(name, []).append((bits, e, w))
+
+    def run(q, call, reads, writes, dma=False):
+        reads, writes = [r[1] for r in reads], [w[1] for w in writes]
+        writes = order(q, reads, writes)
+        if dma:
+            sem, inc = "dma%d" % ndma[0], 16
+            ndma[0] += 1
+        else:
+            sem, inc = counter[q], 1
+        call().then_inc(T.sem[sem], inc)
+        note(reads, writes, sem, inc, known[q])
+
+    def ind(win, offs):
+        return win[0].indirect(offs[0])
+
+    def isap(s):
+        return isinstance(s, tuple)
+
+    def raw(s):
+        return s[0] if isap(s) else s
+
+    def copy(out, in_, offs=None):
+        src = ind(in_, offs) if offs else in_[0]
+        run("v", lambda: g.vector.tensor_copy(out[0], src), [in_] + ([offs] if offs else []), [out])
+
+    def scatter(win, offs, in_):
+        run("v", lambda: g.vector.tensor_copy(ind(win, offs), in_[0]), [in_, offs, win], [win])
+
+    def ts(out, in_, s1, op0, s2=None, op1=None, offs=None):
+        src = ind(in_, offs) if offs else in_[0]
+        reads = [in_] + [s for s in (s1, s2, offs) if isap(s)]
+        if op1 is None:
+            run("v", lambda: g.vector.tensor_scalar(out[0], src, raw(s1), None, op0), reads, [out])
+        else:
+            run("v", lambda: g.vector.tensor_scalar(out[0], src, raw(s1), raw(s2), op0, op1), reads, [out])
+
+    def act(out, in_, fn, bias=None, scale=None, acc=None, offs=None):
+        src = ind(in_, offs) if offs else in_[0]
+        kw = {}
+        if bias is not None:
+            kw["bias"] = raw(bias)
+        if scale is not None:
+            kw["scale"] = raw(scale)
+        if acc:
+            kw["accum_out"] = acc[0]
+        run("s", lambda: g.scalar.activation(out[0], src, fn, **kw),
+            [in_] + [s for s in (bias, scale, offs) if isap(s)], [out] + ([acc] if acc else []))
+
+    def move(q, out, in_, offs=None):
+        if q == "v":
+            copy(out, in_, offs)
+        else:
+            act(out, in_, Fn.Copy, offs=offs)
+
+    def fill(name, a, value):
+        if a < SCRATCH[name][1][1]:
+            out = at(name, a)
+            run("v", lambda: g.vector.memset(out[0], value), [], [out])
+
+    def scan(out, d0, d1, op0, op1):
+        run("v", lambda: g.vector.tensor_tensor_scan(out[0], d0[0], d1[0], 0.0, op0, op1), [d0, d1], [out])
+
+    def quant(name, a, tile):
+        n = tile[0].shape[1] // 4
+        q, s = at("q" + name, a, a + n), at("s" + name, a, a + n)
+        run("v", lambda: g.vector.quantize_mx(q[0], s[0], tile[0]), [tile], [q, s])
+
+    def mm(bank, wname, wa, xname, xa, n=MINC):
+        out = at("ps", 512 * bank, 512 * bank + n)
+        ops = [at("q" + wname, wa, wa + 128), at("s" + wname, wa, wa + 128),
+               at("q" + xname, xa, xa + n), at("s" + xname, xa, xa + n)]
+        run("t", lambda: g.tensor.matmul_mx(out[0], ops[0][0], ops[1][0], ops[2][0], ops[3][0], True, True), ops, [out])
+
+    def load(q, out, src, codes=False):
+        dst = out[0].bitcast(dt.uint8) if codes else out[0]
+        run(q, lambda: queue[q].dma_start(dst, src), [], [out], dma=True)
+
+    def store(q, dst, in_, codes=False):
+        src = in_[0].bitcast(dt.uint8) if codes else in_[0]
+        run(q, lambda: queue[q].dma_start(dst, src), [in_], [], dma=True)
+
+    def iota(out, pattern, cm, small=True):
+        kw = {"allow_small_or_imprecise_dtypes": True} if small else {}
+        run("g", lambda: g.iota(out[0], pattern, 0, cm, **kw), [], [out])
+
+    partners = [T.cores[rank ^ (1 << t)] for t in range(ROUNDS)]
+    mask = topo.mask(core, partners[0])
+    for p in partners:
+        mask &= topo.mask(core, p)
+    lanes = bin(mask).count("1")
+
+    def send(t, k, name, a, land, n):
+        rid, pid = topo.addr(partners[t], core)
+        sem = "arr%d" % k
+        src = [at("q" + name, a, a + n), at("s" + name, a, a + n)]
+        dst = [at("ql", land, land + n), at("sl", land, land + n)]
+        order("g", [s[1] for s in src], [])
+        g.remote_dma(dst[0][0].bitcast(dt.uint8), src[0][0].bitcast(dt.uint8), T.sem[sem], T.sem.sent, pid, rid, mask)
+        g.remote_dma(dst[1][0], src[1][0], T.sem[sem], T.sem.sent, pid, rid, mask)
+        total["sent"] = total.get("sent", 0) + 2 * lanes
+        note([], [d[1] for d in dst], sem, 2 * lanes, {})
+
+    def slot(k, n=1):
+        return at("maps", C * k, C * (k + n))
+
+    def col(name, k):
+        return at(name, k, k + 1)
+
+    load("y", at("lst", LM, LD), T.m[:])
+    load("s", at("lst", LA, LB), T.la[:])
+    load("y", at("lst", LB, LI), T.lb[:])
+    load("y", at("fil", 0, 4 * C), T.x[:])
+    load("y", at("qw"), T.wc[:], codes=True)
+    load("y", at("sw"), T.ws[:])
+    load("y", at("lst", LD, LA), T.ld[:])
+    load("y", at("ut"), T.u[:])
+    load("y", at("vt"), T.v[:])
+
+    iota(at("pcol"), [[0, 1]], 1, small=False)
+    iota(at("k4"), [[1, 4]], 0)
+    iota(at("cnt"), [[1, ROUNDS * A]], 0)
+    iota(at("c16"), [[16, 28]], 0)
+    fill("zero", 0, 0.0)
+    fill("ones", 0, 1.0)
+    run("g", lambda: g.affine_select(T.unit[:], T.ones[:], [[1, 2], [-1, 516]], Op.is_equal, 0.0, 2, 4),
+        [at("ones")], [at("unit")])
+    ts(col("ci", 0), at("pcol"), 15, Op.bitwise_and, 2, Op.logical_shift_right)
+    ts(col("ci", 1), at("pcol"), 3, Op.bitwise_and)
+    ts(col("ci", 2), at("pcol"), 15, Op.bitwise_and)
+    ts(col("ci", 3), at("pcol"), 7, Op.bitwise_and)
+    ts(col("ci", 4), at("pcol"), 4, Op.logical_shift_right)
+    fill("za", 4 * NA, 0.0)
+    copy(at("cf", 0, 5), at("ci", 0, 5))
+    fill("zb", 4 * NB, 0.0)
+    ts(at("c4", 0, 4), at("k4"), col("cf", 0), Op.is_gt, RAMP + DROP, Op.mult)
+    ts(col("addc", 0), col("cf", 0), 4 * RAMP, Op.mult, -12 * RAMP, Op.add)
+    ts(at("c4", 4, 8), at("c4", 0, 4), -DROP, Op.add)
+    ts(col("addc", 1), col("addc", 0), col("cf", 1), Op.add)
+    fill("hb", 4 * NB, 0.0)
+    fill("ha", 4 * NA, 0.0)
+    fill("tiny", 0, TINY)
+    act(at("sgn", 0, 2 * A, 2), at("zero", 0, A), Fn.Copy)
+    for k in range(4):
+        act(at("cpat", k, C, 4), at("zero", 0, C // 4), Fn.Identity, bias=col("c4", 4 + k))
+
+    copy(at("lu", LM, LD), at("lst", LM, LD))
+    act(at("maps", C + 224, 2 * C), at("cnt", 0, C), Fn.Copy, offs=at("lu", LM + 14, LD))
+    copy(at("maps", C, C + 224), at("cnt", 0, C), offs=at("lu", LM, LM + 14))
+    copy(at("lu", LA, LI), at("lst", LA, LI))
+
+    def places(win, lists, t):
+        act(at("row", A, 2 * A), win, Fn.Copy, offs=at(lists, LB + 12 * t, LB + 12 * t + 12))
+        copy(at("row", 0, A), win, offs=at(lists, LA + 12 * t, LA + 12 * t + 12))
+
+    def offsets():
+        scan(at("scn"), at("cpat", 0, 2 * A), at("row"), Op.add, Op.max)
+        ts(at("off", 0, 96), at("scn", 3, 2 * A, 4), 4.0, Op.mult, col("addc", 1), Op.add)
+
+    places(slot(1), "lu", 0)
+    act(slot(0), slot(1), Fn.Copy)
+    offsets()
+
+    def layer(xname, xa, tile, n, skip, width):
+        for b in (2, 0, 3, 1):
+            mm(b, "w", 128 * b, xname, xa, width)
+        for b in (2, 0, 3, 1):
+            out, src = at(tile, b, 4 * n, 4), at("ps", 512 * b + skip, 512 * b + skip + n)
+            if b < 2:
+                ts(out, src, 0.0, Op.max, 0.015625, Op.mult)
+            else:
+                act(out, src, Fn.Relu, scale=0.015625)
+
+    for t in range(ROUNDS):
+        new = C + A * t
+        win = at("fil", 0, 4 * new)
+        la_, lb_ = MINC + A * t, MINC + A * t + NA
+        base = 2 * t
+
+        ca = NA // 4
+        cuts = list(zip(ZCUT[:-1], ZCUT[1:]))
+        for c0, c1 in [cuts[1], cuts[0]] + cuts[2:]:
+            move("s" if c0 else "v", at("opb", 16 * c0, 16 * c1), win, at("off", 48 + c0, 48 + c1))
+        for c0, c1 in cuts:
+            tile, first = ("za", 0) if c0 < ca else ("zb", ca)
+            out, offs, b = at(tile, 16 * (c0 - first), 16 * (c1 - first)), at("off", c0, c1), at("opb", 16 * c0, 16 * c1)
+            run("v", lambda: g.vector.tensor_tensor(out[0], ind(win, offs), b[0], Op.add), [win, offs, b], [out])
+            if c1 == ca:
+                quant("za", MINC * t, at("za"))
+                send(t, 2 * t, "za", MINC * t, la_, NA)
+        quant("zb", 0, at("zb"))
+        if t == 0:
+            act(at("cand", 0, ROUNDS * 2 * A, 2), at("cnt"), Fn.Identity, bias=float(C))
+        else:
+            act(slot(base), slot(t - 1, 2), Fn.Copy, offs=at("lsh", LI, LS))
+        layer("zb", 0, "hb", NB, 0, WB)
+        quant("hb", WB * t, at("hb"))
+        send(t, 2 * t + 1, "hb", WB * t, lb_, NB)
+
+        if t == 0:
+            act(at("c32"), at("zero", 0, 32), Fn.Identity, bias=col("cf", 3))
+            act(at("ids", 0, LS - LI), at("c16"), Fn.Identity, bias=col("cf", 2))
+            copy(at("lu", LD, LA), at("lst", LD, LA))
+            quant("l", 0, at("zero"))
+            quant("u", 0, at("ut"))
+            copy(at("upick", 0, 8), at("c16", 0, 8))
+            ts(at("upick", 8, 16), at("c32", 0, 8), 16.0, Op.mult)
+            act(at("ids", LS - LI), at("ids", 0, 8), Fn.Identity, scale=4.0, bias=3.0)
+        act(at("cand", 2 * A * t + 1, 2 * A * (t + 1), 2), slot(base), Fn.Copy, offs=at("lu", LD + 12 * t, LD + 12 * t + 12))
+        if t == 0:
+            run("v", lambda: g.vector.tensor_copy(T.qp[:, 0:256].bitcast(dt.uint32),
+                                                  T.qu[:, 0:128].bitcast(dt.uint32).indirect(T.upick[:, 0:16])),
+                [at("qu"), at("upick")], [at("qp")])
+            act(at("sp", 0, 256), at("su", 0, 128), Fn.Copy, offs=at("upick", 0, 16))
+            for b in range(4):
+                a = 516 * (b % 2) + 2 - 2 * (b // 2)
+                quant("e", 128 * b, at("unit", a, a + 512))
+            ts(at("tie", 0, 32), at("c32"), 0.125, Op.mult)
+            ts(col("tie", 32), col("cf", 4), 0.125, Op.mult)
+            ts(at("lf", LA, LI), at("lst", LA, LI), HALF + 0.25, Op.add, 1.0 / HALF, Op.mult)
+            ts(at("lf", LI, LE), at("ids"), HALF + 0.25, Op.add, 1.0 / HALF, Op.mult)
+        if t == 1:
+            act(slot(3), slot(2), Fn.Copy)
+            quant("v", 0, at("vt"))
+        if t == 2:
+            scan(at("sel", 0, C), at("cpat"), slot(3), Op.add, Op.max)
+
+        def scores(part, bank, j0, n, skip):
+            p = 512 * bank + skip
+            act(at("sgn", 2 * j0 + 1, 2 * (j0 + n), 2), at("ps", p, p + n), Fn.Sign, bias=at("tiny"), acc=col("acc", part))
+            act(at("junk", 0, n), at("ps", p + 512, p + 512 + n), Fn.Sign, bias=at("tiny"), acc=col("acc", 2 + part))
+
+        def choose(j0, n):
+            scan(at("nv", 2 * j0, 2 * (j0 + n)), at("sgn", 2 * j0, 2 * (j0 + n)),
+                 at("cand", 2 * (A * t + j0), 2 * (A * t + j0 + n)), Op.mult, Op.max)
+
+        def commit(j0, n):
+            c = LD + 12 * t + j0 // 16
+            scatter(slot(base), at("lu", c, c + n // 16), at("nv", 2 * j0 + 1, 2 * (j0 + n), 2))
+
+        def unpack(b, q, j0, n, skip):
+            move(q, at("fil", 4 * (new + j0) + b, 4 * (new + j0 + n), 4), at("ps", 512 * b + skip, 512 * b + skip + n))
+
+        own = col("tie", 32)
+        if NA:
+            layer("l", la_ + NA - MINC, "ha", NA, MINC - NA, MINC)
+            quant("ga", 0, at("ha"))
+            mm(4, "p", 0, "ga", 0)
+            mm(0, "e", 0, "ga", 0)
+            mm(5, "p", 128, "ga", 0)
+            for b in (2, 1, 3):
+                mm(b, "e", 128 * b, "ga", 0)
+            unpack(0, "v", 0, NA, 0)
+            scores(0, 4, 0, NA, 0)
+            choose(0, NA)
+            unpack(1, "v", 0, NA, 0)
+            unpack(2, "s", 0, NA, 0)
+            commit(0, NA)
+            unpack(3, "s", 0, NA, 0)
+            act(col("acc", 4), own, Fn.Identity, bias=col("acc", 0))
+            own = col("acc", 4)
+
+        xa, skip = lb_ + NB - WB, WB - NB
+        mm(6, "p", 0, "l", xa, WB)
+        mm(0, "e", 0, "l", xa, WB)
+        mm(7, "p", 128, "l", xa, WB)
+        for b in (1, 2, 3):
+            mm(b, "e", 128 * b, "l", xa, WB)
+        unpack(0, "v", NA, NB, skip)
+        scores(1, 6, NA, NB, skip)
+        choose(NA, NB)
+        act(col("acc", 5), own, Fn.Identity, bias=col("acc", 1))
+        if NA:
+            ts(at("key", 0, 32), at("tie", 0, 32), col("acc", 2), Op.add, col("acc", 3), Op.add)
+        else:
+            ts(at("key", 0, 32), at("tie", 0, 32), col("acc", 3), Op.add)
+        run("v", lambda: g.vector.transpose(T.key[:, 32:64], T.key[:, 0:32]), [at("key", 0, 32)], [at("key", 32, 64)])
+        unpack(1, "s", NA, NB, skip)
+        commit(NA, NB)
+        act(at("cmp"), at("key", 32, 40), Fn.Sign, scale=-1.0, bias=col("acc", 5), acc=col("acc", 6))
+        side = -1.0 if t == 0 else 1.0
+        act(at("keep"), col("acc", 6), Fn.Sign, scale=side, bias=4.0 * side)
+        unpack(2, "s", NA, NB, skip)
+        if t < ROUNDS - 1:
+            a = LA + 12 * (t + 1)
+            ts(at("lsh", a, LS), at("lf", a, LS), at("keep"), Op.add, HALF, Op.mult)
+            places(slot(t, 2), "lsh", t + 1)
+            unpack(3, "s", NA, NB, skip)
+            offsets()
+        else:
+            ts(at("lsh", LI, LE), at("lf", LI, LE), at("keep"), Op.add, HALF, Op.mult)
+            unpack(3, "s", NA, NB, skip)
+            scan(at("sel", C, 2 * C), at("cpat"), slot(4), Op.add, Op.max)
+            ts(at("off"), at("sel"), 4.0, Op.mult, col("addc", 1), Op.add, offs=at("lsh", LS, LS + 7))
+            act(at("omr"), slot(3, 2), Fn.Copy, offs=at("lsh", LI, LS))
+
+    store("y", T.om[:], at("omr", rows=slice(0, 128, 16)))
+    win = at("fil")
+    runs = len(TCUT) - 1
+
+    def result(k, q):
+        a, b = TCUT[k], TCUT[k + 1]
+        move(q, at("ysb", a, b), at("ps", 512 * k, 512 * k + b - a))
+        store("s" if q == "s" else "y", T.y[:, a:b], at("ysb", a, b))
+
+    for k in range(runs):
+        c0, c1 = TCUT[k] // 4, TCUT[k + 1] // 4
+        cm = c0 + TSHARE[k]
+        act(at("tt", 16 * cm, 16 * c1), win, Fn.Copy, offs=at("off", cm, c1))
+        copy(at("tt", 16 * c0, 16 * cm), win, offs=at("off", c0, cm))
+        if k:
+            result(k - 1, "s")
+        a, b = TCUT[k], TCUT[k + 1]
+        quant("t", a, at("tt", 4 * a, 4 * b))
+        store("y", T.oc[:, 4 * a:4 * b], at("qt", a, b), codes=True)
+        mm(k, "v", 0, "t", a, b - a)
+    for i in range(4):
+        store("s" if i > 0 else "y", T.osc[4 * i:4 * i + 4, :], at("st", rows=slice(32 * i, 32 * i + 4)))
+    result(runs - 1, "v")
+    for sem, n in total.items():
+        g.wait_ge(T.sem[sem], n)

@@ -1,30 +1,39 @@
 from concourse.mybir import dt, AluOpType as Op, ActivationFunctionType as Fn
 
 C, A, ROUNDS = 448, 192, 3
-NA = 96
-NB = A - NA
+NAS = [64, 96, 96]
 MINC = 128
-WB = max(MINC, NB)
 RAMP, DROP = 2048.0, 65536.0
 TINY = 2.0 ** -126
 HALF = C / 2
-ZCUT = [0, 8, 24, 48]
-TCUT = [0, 256, 448]
-TSHARE = [36, 20]
+ZCUT = [[0, 8, 16, 32, 48], [0, 12, 24, 36, 48], [0, 12, 24, 36, 48]]
+TCUT = [0, 160, 320, 448]
+TG = [0, 32, 40, 66, 80, 100, 112]
+CCUT = [0, 160, 320, 448]
+YCUT = [0, 160, 320, 448]
+T1 = 128
+WIDE = [False, False, False]
 LAND = MINC + ROUNDS * A
 F32, BF, I32, U16, Q4, U8 = "float32", "bfloat16", "int32", "uint16", "float8_e4m3fn_x4", "uint8"
-LM, LD, LA, LB, LI, LS, LE = 0, 28, 64, 100, 136, 164, 172
+LM, LA, LB, LD, LI, LS, LE = 0, 28, 64, 100, 136, 164, 172
+ORDER = """
+pcol za0 Lm La Lb Lx Lwc k8 tiny Lu ci1 Lws Ld ci0 cnt zero cfa ci3 c4a adc0 c4b ones cpat2+ cpat0+ lum ha0 cpat3+ unit0 adc1 map1 map0 lul cpat1+ ci4 ci2 lkb0_0- lkb1_0+ cfb lka0_0+ scb_0 unit1 lka1_0+ zb0 ofb_0 sca_0 hb0 ofa_0 up1 gb0_0+ gb1_0+ ga0_0 gb2_0+ ga1_0 up0 qza_0 gb3_0+ ga2_0 sndA_0 sgn0+ ga3_0 cnew_0+ slot_0+ ids0 tie0 qzb_0 ids1 mw3B_0 ql0 mw2B_0 tie1 ev3B_0+ qu mw0B_0 mw1B_0 ev2B_0- ev1B_0+ lud tie2 qe0 ev0B_0+ lf1 pks qhb_0 qe2 sndB_0 pkq mw2A_0 mw0A_0 ev2A_0+ mw1A_0 ev0A_0+ mw3A_0 ev1A_0+ ev3A_0- cold_0+ qga_0 qe3 moA_0 qe1 mmA_0 soA_0 me0A_0 lf0 smA_0 me2A_0 un0A_0- me3A_0 Lv un2A_0+ chA_0 moB_0 kea_0+ mmB_0 un3A_0- soB_0 me0B_0 cmA_0 me2B_0 smB_0 me1A_0 chB_0 me3B_0 un2B_0+ key_0+ un1A_0- un0B_0+ own_0- me1B_0 tr_0 cmB_0 cmp_0 un1B_0+ keep_0 un3B_0+ lsh_0
+lkb1_1+ lkb0_1- lsi_0 lka1_1+ scb_1 lka0_1+ ofb_1 gb0_1+ sca_1 ofa_1 gb1_1+ ga0_1 gb2_1+ ga1_1 gb3_1+ qza_1 ga2_1 sndA_1 slot_1+ ga3_1 qzb_1 slot3+ mw0B_1 mw2B_1 ev0B_1- mw3B_1 ev2B_1- mw1B_1 ev3B_1+ ev1B_1- qhb_1 sndB_1 mw0A_1 mw2A_1 ev0A_1+ mw3A_1 ev2A_1- mw1A_1 ev3A_1+ ev1A_1- cold_1+ qga_1 cnew_1- moA_1 me0A_1 soA_1 qv me1A_1 un0A_1- mmA_1 un1A_1+ me3A_1 chA_1 me2A_1 smA_1 un3A_1- un2A_1+ kea_1- moB_1 cmA_1 mmB_1 soB_1 me0B_1 me1B_1 smB_1 me2B_1 chB_1 me3B_1 key_1+ own_1- un2B_1+ tr_1 cmB_1 cmp_1 keep_1 un3B_1+ lsh_1 un0B_1+
+lkb0_2- lkb1_2+ un1B_1- lka0_2+ scb_2 lka1_2+ ofb_2 sca_2 gb0_2+ ofa_2 lsi_1 gb1_2+ ga0_2 gb2_2+ ga1_2 gb3_2+ qza_2 ga2_2 sndA_2 slot_2+ ga3_2 qzb_2 cnew_2+ selrb mw2B_2 mw0B_2 ev2B_2+ mw3B_2 mw1B_2 ev0B_2+ ev1B_2- ev3B_2+ qhb_2 sndB_2 mw1A_2 mw3A_2 ev1A_2- mw2A_2 ev3A_2+ mw0A_2 ev2A_2+ ev0A_2- cold_2+ qga_2 moA_2 me0A_2 soA_2 mmA_2 un0A_2- me2A_2 smA_2 chA_2 me3A_2 me1A_2 kea_2+ un3A_2- un2A_2+ cmA_2 moB_2 mmB_2 soB_2 me3B_2 un1A_2- me0B_2 smB_2 me2B_2 chB_2 own_2+ me1B_2 key_2+ un0B_2+ tr_2 cmB_2 cmp_2 keep_2 un1B_2+ lsh_2 un2B_2+
+selA un3B_2+ ofA selB gt0+ ofB gt1- gt2+ qt0 gt3- Sc0- my0 ey0- gt4+ qt1 Sy0- gt5- Sc1- my1 om0+ qt2 ey1- my2 Sc2- Ss0+ Ss1- Ss2+ Ss3- ey2+ om1- Sy1- Sy2- So+
+"""
+ENG = {n[:-1]: "s" if n[-1] == "+" else "vy"[n[0] == "S"] for n in ORDER.split() if n[-1] in "+-"}
 
 SCRATCH = {
     "lst": ("sbuf", [128, LI], I32), "lu": ("sbuf", [128, LI], U16), "ids": ("sbuf", [128, LE - LI], F32),
     "lf": ("sbuf", [128, LE], F32), "lsh": ("sbuf", [128, LE], U16),
     "fil": ("sbuf", [128, 4096], BF), "maps": ("sbuf", [128, 5 * C], F32),
-    "cnt": ("sbuf", [128, ROUNDS * A], F32), "pcol": ("sbuf", [128, 1], I32), "k4": ("sbuf", [128, 4], F32),
-    "c16": ("sbuf", [128, 28], F32), "ci": ("sbuf", [128, 8], I32), "cf": ("sbuf", [128, 8], F32),
+    "cnt": ("sbuf", [128, C], F32), "pcol": ("sbuf", [128, 1], I32), "k8": ("sbuf", [128, 8], F32),
+    "ci": ("sbuf", [128, 8], I32), "cf": ("sbuf", [128, 8], F32),
     "c4": ("sbuf", [128, 8], F32), "addc": ("sbuf", [128, 2], F32), "tiny": ("sbuf", [128, 1], F32),
-    "cpat": ("sbuf", [128, C], F32), "c32": ("sbuf", [128, 32], F32), "upick": ("sbuf", [128, 16], U16),
-    "tie": ("sbuf", [128, 36], F32),
-    "zero": ("sbuf", [128, 512], BF), "ones": ("sbuf", [128, 1032], BF), "unit": ("sbuf", [128, 1032], BF),
+    "cpat": ("sbuf", [128, C], F32), "upick": ("sbuf", [128, 16], U16),
+    "tie": ("sbuf", [128, 68], F32),
+    "zero": ("sbuf", [128, 512], BF), "ones": ("sbuf", [128, 516], BF), "unit": ("sbuf", [128, 1032], BF),
     "qe": ("sbuf", [128, 512], Q4), "se": ("sbuf", [128, 512], U8),
     "qw": ("sbuf", [128, 512], Q4), "sw": ("sbuf", [128, 512], U8),
     "ut": ("sbuf", [128, 512], BF), "vt": ("sbuf", [128, 512], BF),
@@ -33,11 +42,11 @@ SCRATCH = {
     "qv": ("sbuf", [128, 128], Q4), "sv": ("sbuf", [128, 128], U8),
     "row": ("sbuf", [128, 2 * A], F32), "scn": ("sbuf", [128, 2 * A], F32), "off": ("sbuf", [128, 112], U16),
     "opb": ("sbuf", [128, 4 * A], BF),
-    "za": ("sbuf", [128, 4 * MINC], BF), "zb": ("sbuf", [128, 4 * WB], BF),
-    "ha": ("sbuf", [128, 4 * MINC], BF), "hb": ("sbuf", [128, 4 * WB], BF),
+    "za": ("sbuf", [128, 4 * MINC], BF), "zb": ("sbuf", [128, 4 * A], BF),
+    "ha": ("sbuf", [128, 4 * MINC], BF), "hb": ("sbuf", [128, 4 * A], BF),
     "qza": ("sbuf", [128, ROUNDS * MINC], Q4), "sza": ("sbuf", [128, ROUNDS * MINC], U8),
-    "qhb": ("sbuf", [128, ROUNDS * WB], Q4), "shb": ("sbuf", [128, ROUNDS * WB], U8),
-    "qzb": ("sbuf", [128, WB], Q4), "szb": ("sbuf", [128, WB], U8),
+    "qhb": ("sbuf", [128, ROUNDS * A], Q4), "shb": ("sbuf", [128, ROUNDS * A], U8),
+    "qzb": ("sbuf", [128, A], Q4), "szb": ("sbuf", [128, A], U8),
     "qga": ("sbuf", [128, MINC], Q4), "sga": ("sbuf", [128, MINC], U8),
     "ql": ("sbuf", [128, LAND], Q4), "sl": ("sbuf", [128, LAND], U8),
     "sgn": ("sbuf", [128, 2 * A], F32), "cand": ("sbuf", [128, ROUNDS * 2 * A], F32), "nv": ("sbuf", [128, 2 * A], F32),
@@ -60,6 +69,7 @@ def rank_program(g, core, T, topo):
     counter = {"v": "nv_", "s": "ns_", "t": "nt_", "g": "ng_"}
     known = {q: {} for q in queue}
     total, log, ndma = {}, {}, [0]
+    steps = {}
 
     def at(name, a=0, b=None, step=1, rows=slice(None)):
         b = SCRATCH[name][1][1] if b is None else b
@@ -90,16 +100,18 @@ def rank_program(g, core, T, topo):
             for name, bits in regs:
                 log.setdefault(name, []).append((bits, e, w))
 
-    def run(q, call, reads, writes, dma=False):
-        reads, writes = [r[1] for r in reads], [w[1] for w in writes]
-        writes = order(q, reads, writes)
-        if dma:
-            sem, inc = "dma%d" % ndma[0], 16
-            ndma[0] += 1
-        else:
-            sem, inc = counter[q], 1
-        call().then_inc(T.sem[sem], inc)
-        note(reads, writes, sem, inc, known[q])
+    def run(name, q, call, reads, writes, dma=False):
+        def emit():
+            r = [x[1] for x in reads]
+            w = order(q, r, [x[1] for x in writes])
+            if dma:
+                sem, inc = "dma%d" % ndma[0], 16
+                ndma[0] += 1
+            else:
+                sem, inc = counter[q], 1
+            call().then_inc(T.sem[sem], inc)
+            note(r, w, sem, inc, known[q])
+        steps[name] = emit
 
     def ind(win, offs):
         return win[0].indirect(offs[0])
@@ -110,22 +122,19 @@ def rank_program(g, core, T, topo):
     def raw(s):
         return s[0] if isap(s) else s
 
-    def copy(out, in_, offs=None):
+    def copy(nm, out, in_, offs=None):
         src = ind(in_, offs) if offs else in_[0]
-        run("v", lambda: g.vector.tensor_copy(out[0], src), [in_] + ([offs] if offs else []), [out])
+        run(nm, "v", lambda: g.vector.tensor_copy(out[0], src), [in_] + ([offs] if offs else []), [out])
 
-    def scatter(win, offs, in_):
-        run("v", lambda: g.vector.tensor_copy(ind(win, offs), in_[0]), [in_, offs, win], [win])
-
-    def ts(out, in_, s1, op0, s2=None, op1=None, offs=None):
+    def ts(nm, out, in_, s1, op0, s2=None, op1=None, offs=None):
         src = ind(in_, offs) if offs else in_[0]
         reads = [in_] + [s for s in (s1, s2, offs) if isap(s)]
         if op1 is None:
-            run("v", lambda: g.vector.tensor_scalar(out[0], src, raw(s1), None, op0), reads, [out])
+            run(nm, "v", lambda: g.vector.tensor_scalar(out[0], src, raw(s1), None, op0), reads, [out])
         else:
-            run("v", lambda: g.vector.tensor_scalar(out[0], src, raw(s1), raw(s2), op0, op1), reads, [out])
+            run(nm, "v", lambda: g.vector.tensor_scalar(out[0], src, raw(s1), raw(s2), op0, op1), reads, [out])
 
-    def act(out, in_, fn, bias=None, scale=None, acc=None, offs=None):
+    def act(nm, out, in_, fn, bias=None, scale=None, acc=None, offs=None):
         src = ind(in_, offs) if offs else in_[0]
         kw = {}
         if bias is not None:
@@ -134,62 +143,71 @@ def rank_program(g, core, T, topo):
             kw["scale"] = raw(scale)
         if acc:
             kw["accum_out"] = acc[0]
-        run("s", lambda: g.scalar.activation(out[0], src, fn, **kw),
+        run(nm, "s", lambda: g.scalar.activation(out[0], src, fn, **kw),
             [in_] + [s for s in (bias, scale, offs) if isap(s)], [out] + ([acc] if acc else []))
 
-    def move(q, out, in_, offs=None):
-        if q == "v":
-            copy(out, in_, offs)
+    def move(nm, q, out, in_, offs=None):
+        if ENG.get(nm, q) == "v":
+            copy(nm, out, in_, offs)
         else:
-            act(out, in_, Fn.Copy, offs=offs)
+            act(nm, out, in_, Fn.Copy, offs=offs)
 
-    def fill(name, a, value):
-        if a < SCRATCH[name][1][1]:
-            out = at(name, a)
-            run("v", lambda: g.vector.memset(out[0], value), [], [out])
+    def plus(nm, q, out, in_, s):
+        if ENG.get(nm, q) == "v":
+            ts(nm, out, in_, s, Op.add)
+        else:
+            act(nm, out, in_, Fn.Identity, bias=s)
 
-    def scan(out, d0, d1, op0, op1):
-        run("v", lambda: g.vector.tensor_tensor_scan(out[0], d0[0], d1[0], 0.0, op0, op1), [d0, d1], [out])
+    def fill(nm, out, value):
+        run(nm, "v", lambda: g.vector.memset(out[0], value), [], [out])
 
-    def quant(name, a, tile):
+    def scan(nm, out, d0, d1, op0, op1):
+        run(nm, "v", lambda: g.vector.tensor_tensor_scan(out[0], d0[0], d1[0], 0.0, op0, op1), [d0, d1], [out])
+
+    def quant(nm, name, a, tile):
         n = tile[0].shape[1] // 4
         q, s = at("q" + name, a, a + n), at("s" + name, a, a + n)
-        run("v", lambda: g.vector.quantize_mx(q[0], s[0], tile[0]), [tile], [q, s])
+        run(nm, "v", lambda: g.vector.quantize_mx(q[0], s[0], tile[0]), [tile], [q, s])
 
-    def mm(bank, wname, wa, xname, xa, n=MINC):
+    def mm(nm, bank, wname, wa, xname, xa, n=MINC):
         out = at("ps", 512 * bank, 512 * bank + n)
         ops = [at("q" + wname, wa, wa + 128), at("s" + wname, wa, wa + 128),
                at("q" + xname, xa, xa + n), at("s" + xname, xa, xa + n)]
-        run("t", lambda: g.tensor.matmul_mx(out[0], ops[0][0], ops[1][0], ops[2][0], ops[3][0], True, True), ops, [out])
+        run(nm, "t", lambda: g.tensor.matmul_mx(out[0], ops[0][0], ops[1][0], ops[2][0], ops[3][0], True, True), ops, [out])
 
-    def load(q, out, src, codes=False):
+    def load(nm, q, out, src, codes=False, after=()):
         dst = out[0].bitcast(dt.uint8) if codes else out[0]
-        run(q, lambda: queue[q].dma_start(dst, src), [], [out], dma=True)
+        run(nm, q, lambda: queue[q].dma_start(dst, src), list(after), [out], dma=True)
 
-    def store(q, dst, in_, codes=False):
+    def store(nm, q, dst, in_, codes=False):
         src = in_[0].bitcast(dt.uint8) if codes else in_[0]
-        run(q, lambda: queue[q].dma_start(dst, src), [in_], [], dma=True)
+        q = ENG.get(nm, q)
+        run(nm, q, lambda: queue[q].dma_start(dst, src), [in_], [], dma=True)
 
-    def iota(out, pattern, cm, small=True):
+    def iota(nm, out, pattern, cm, small=True):
         kw = {"allow_small_or_imprecise_dtypes": True} if small else {}
-        run("g", lambda: g.iota(out[0], pattern, 0, cm, **kw), [], [out])
+        run(nm, "g", lambda: g.iota(out[0], pattern, 0, cm, **kw), [], [out])
 
     partners = [T.cores[rank ^ (1 << t)] for t in range(ROUNDS)]
-    mask = topo.mask(core, partners[0])
+    common = topo.mask(core, partners[0])
     for p in partners:
-        mask &= topo.mask(core, p)
-    lanes = bin(mask).count("1")
+        common &= topo.mask(core, p)
 
-    def send(t, k, name, a, land, n):
+    def send(nm, t, k, name, a, land, n):
         rid, pid = topo.addr(partners[t], core)
+        mask = topo.mask(core, partners[t]) if WIDE[t] else common
+        lanes = bin(mask).count("1")
         sem = "arr%d" % k
         src = [at("q" + name, a, a + n), at("s" + name, a, a + n)]
         dst = [at("ql", land, land + n), at("sl", land, land + n)]
-        order("g", [s[1] for s in src], [])
-        g.remote_dma(dst[0][0].bitcast(dt.uint8), src[0][0].bitcast(dt.uint8), T.sem[sem], T.sem.sent, pid, rid, mask)
-        g.remote_dma(dst[1][0], src[1][0], T.sem[sem], T.sem.sent, pid, rid, mask)
-        total["sent"] = total.get("sent", 0) + 2 * lanes
-        note([], [d[1] for d in dst], sem, 2 * lanes, {})
+
+        def emit():
+            order("g", [s[1] for s in src], [])
+            g.remote_dma(dst[0][0].bitcast(dt.uint8), src[0][0].bitcast(dt.uint8), T.sem[sem], T.sem.sent, pid, rid, mask)
+            g.remote_dma(dst[1][0], src[1][0], T.sem[sem], T.sem.sent, pid, rid, mask)
+            total["sent"] = total.get("sent", 0) + 2 * lanes
+            note([], [d[1] for d in dst], sem, 2 * lanes, {})
+        steps[nm] = emit
 
     def slot(k, n=1):
         return at("maps", C * k, C * (k + n))
@@ -197,215 +215,227 @@ def rank_program(g, core, T, topo):
     def col(name, k):
         return at(name, k, k + 1)
 
-    load("y", at("lst", LM, LD), T.m[:])
-    load("s", at("lst", LA, LB), T.la[:])
-    load("y", at("lst", LB, LI), T.lb[:])
-    load("y", at("fil", 0, 4 * C), T.x[:])
-    load("y", at("qw"), T.wc[:], codes=True)
-    load("y", at("sw"), T.ws[:])
-    load("y", at("lst", LD, LA), T.ld[:])
-    load("y", at("ut"), T.u[:])
-    load("y", at("vt"), T.v[:])
+    load("Lm", "y", at("lst", LM, LA), T.m[:])
+    load("La", "s", at("lst", LA, LB), T.la[:])
+    load("Lb", "y", at("lst", LB, LD), T.lb[:])
+    load("Lx", "y", at("fil", 0, 4 * C), T.x[:])
+    load("Lwc", "y", at("qw"), T.wc[:], codes=True)
+    load("Lws", "y", at("sw"), T.ws[:])
+    load("Ld", "y", at("lst", LD, LI), T.ld[:])
+    load("Lu", "y", at("ut"), T.u[:])
 
-    iota(at("pcol"), [[0, 1]], 1, small=False)
-    iota(at("k4"), [[1, 4]], 0)
-    iota(at("cnt"), [[1, ROUNDS * A]], 0)
-    iota(at("c16"), [[16, 28]], 0)
-    fill("zero", 0, 0.0)
-    fill("ones", 0, 1.0)
-    run("g", lambda: g.affine_select(T.unit[:], T.ones[:], [[1, 2], [-1, 516]], Op.is_equal, 0.0, 2, 4),
-        [at("ones")], [at("unit")])
-    ts(col("ci", 0), at("pcol"), 15, Op.bitwise_and, 2, Op.logical_shift_right)
-    ts(col("ci", 1), at("pcol"), 3, Op.bitwise_and)
-    ts(col("ci", 2), at("pcol"), 15, Op.bitwise_and)
-    ts(col("ci", 3), at("pcol"), 7, Op.bitwise_and)
-    ts(col("ci", 4), at("pcol"), 4, Op.logical_shift_right)
-    fill("za", 4 * NA, 0.0)
-    copy(at("cf", 0, 5), at("ci", 0, 5))
-    fill("zb", 4 * NB, 0.0)
-    ts(at("c4", 0, 4), at("k4"), col("cf", 0), Op.is_gt, RAMP + DROP, Op.mult)
-    ts(col("addc", 0), col("cf", 0), 4 * RAMP, Op.mult, -12 * RAMP, Op.add)
-    ts(at("c4", 4, 8), at("c4", 0, 4), -DROP, Op.add)
-    ts(col("addc", 1), col("addc", 0), col("cf", 1), Op.add)
-    fill("hb", 4 * NB, 0.0)
-    fill("ha", 4 * NA, 0.0)
-    fill("tiny", 0, TINY)
-    act(at("sgn", 0, 2 * A, 2), at("zero", 0, A), Fn.Copy)
+    iota("pcol", at("pcol"), [[0, 1]], 1, small=False)
+    iota("k8", at("k8"), [[1, 8]], 0)
+    iota("cnt", at("cnt"), [[1, C]], 0)
+    fill("tiny", at("tiny"), TINY)
+    fill("za0", at("za", 4 * min(NAS)), 0.0)
+    ts("ci0", col("ci", 0), at("pcol"), 15, Op.bitwise_and, 2, Op.logical_shift_right)
+    ts("ci1", col("ci", 1), at("pcol"), 3, Op.bitwise_and)
+    ts("ci2", col("ci", 2), at("pcol"), 15, Op.bitwise_and)
+    copy("cfa", at("cf", 0, 2), at("ci", 0, 2))
+    ts("ci3", col("ci", 3), at("pcol"), 7, Op.bitwise_and)
+    ts("c4a", at("c4", 0, 4), at("k8", 0, 4), col("cf", 0), Op.is_gt, RAMP + DROP, Op.mult)
+    ts("ci4", col("ci", 4), at("pcol"), 5, Op.logical_shift_right)
+    ts("c4b", at("c4", 4, 8), at("c4", 0, 4), -DROP, Op.add)
+    fill("zero", at("zero"), 0.0)
     for k in range(4):
-        act(at("cpat", k, C, 4), at("zero", 0, C // 4), Fn.Identity, bias=col("c4", 4 + k))
+        plus("cpat%d" % k, "s", at("cpat", k, C, 4), at("zero", 0, C // 4), col("c4", 4 + k))
+    fill("ones", at("ones"), 1.0)
+    ts("adc0", col("addc", 0), col("cf", 0), 4 * RAMP, Op.mult, -12 * RAMP, Op.add)
+    copy("cfb", at("cf", 2, 5), at("ci", 2, 5))
+    ts("adc1", col("addc", 1), col("addc", 0), col("cf", 1), Op.add)
+    if A - max(NAS) < MINC:
+        fill("zb0", at("zb", 4 * (A - max(NAS)), 4 * MINC), 0.0)
+        fill("hb0", at("hb", 4 * (A - max(NAS)), 4 * MINC), 0.0)
+    fill("ha0", at("ha", 4 * min(NAS)), 0.0)
 
-    copy(at("lu", LM, LD), at("lst", LM, LD))
-    act(at("maps", C + 224, 2 * C), at("cnt", 0, C), Fn.Copy, offs=at("lu", LM + 14, LD))
-    copy(at("maps", C, C + 224), at("cnt", 0, C), offs=at("lu", LM, LM + 14))
-    copy(at("lu", LA, LI), at("lst", LA, LI))
+    def unit(i):
+        out = at("unit", 516 * i, 516 * (i + 1))
+        run("unit%d" % i, "g", lambda: g.affine_select(out[0], T.ones[:], [[-1, 516]], Op.is_equal, 0.0, 2 + i, 4),
+            [at("ones")], [out])
+    unit(0)
+
+    copy("lum", at("lu", LM, LA), at("lst", LM, LA))
+    copy("map0", at("maps", C, C + 192), at("cnt"), offs=at("lu", LM, LM + 12))
+    act("map1", at("maps", C + 192, 2 * C), at("cnt"), Fn.Copy, offs=at("lu", LM + 12, LA))
+    copy("lul", at("lu", LA, LB + 12), at("lst", LA, LB + 12))
 
     def places(win, lists, t):
-        act(at("row", A, 2 * A), win, Fn.Copy, offs=at(lists, LB + 12 * t, LB + 12 * t + 12))
-        copy(at("row", 0, A), win, offs=at(lists, LA + 12 * t, LA + 12 * t + 12))
-
-    def offsets():
-        scan(at("scn"), at("cpat", 0, 2 * A), at("row"), Op.add, Op.max)
-        ts(at("off", 0, 96), at("scn", 3, 2 * A, 4), 4.0, Op.mult, col("addc", 1), Op.add)
+        for o, l, r in (("b", LB, A), ("a", LA, 0)):
+            for h in range(2):
+                move("lk%s%d_%d" % (o, h, t), "v" if (o, h) == ("b", 0) else "s", at("row", r + 96 * h, r + 96 * h + 96), win,
+                     at(lists, l + 12 * t + 6 * h, l + 12 * t + 6 * h + 6))
+        for o, r in (("b", A), ("a", 0)):
+            scan("sc%s_%d" % (o, t), at("scn", r, r + A), at("cpat", 0, A), at("row", r, r + A), Op.add, Op.max)
+            ts("of%s_%d" % (o, t), at("off", r // 4, r // 4 + 48), at("scn", r + 3, r + A, 4), 4.0, Op.mult, col("addc", 1), Op.add)
 
     places(slot(1), "lu", 0)
-    act(slot(0), slot(1), Fn.Copy)
-    offsets()
 
-    def layer(xname, xa, tile, n, skip, width):
+    def layer(tag, xname, xa, tile, n, skip, width):
         for b in (2, 0, 3, 1):
-            mm(b, "w", 128 * b, xname, xa, width)
+            mm("mw%d%s" % (b, tag), b, "w", 128 * b, xname, xa, width)
         for b in (2, 0, 3, 1):
-            out, src = at(tile, b, 4 * n, 4), at("ps", 512 * b + skip, 512 * b + skip + n)
-            if b < 2:
-                ts(out, src, 0.0, Op.max, 0.015625, Op.mult)
+            out, src, nm = at(tile, b, 4 * n, 4), at("ps", 512 * b + skip, 512 * b + skip + n), "ev%d%s" % (b, tag)
+            if ENG.get(nm, "v" if b < 2 else "s") == "v":
+                ts(nm, out, src, 0.0, Op.max, 0.015625, Op.mult)
             else:
-                act(out, src, Fn.Relu, scale=0.015625)
+                act(nm, out, src, Fn.Relu, scale=0.015625)
 
-    for t in range(ROUNDS):
+    def one_round(t):
+        NA = NAS[t]
+        NB = A - NA
+        WB = max(MINC, NB)
         new = C + A * t
         win = at("fil", 0, 4 * new)
         la_, lb_ = MINC + A * t, MINC + A * t + NA
         base = 2 * t
+        tag = "_%d" % t
 
         ca = NA // 4
-        cuts = list(zip(ZCUT[:-1], ZCUT[1:]))
-        for c0, c1 in [cuts[1], cuts[0]] + cuts[2:]:
-            move("s" if c0 else "v", at("opb", 16 * c0, 16 * c1), win, at("off", 48 + c0, 48 + c1))
-        for c0, c1 in cuts:
+        cuts = list(zip(ZCUT[t][:-1], ZCUT[t][1:]))
+        for i, (c0, c1) in enumerate(cuts):
+            move("gb%d%s" % (i, tag), "s", at("opb", 16 * c0, 16 * c1), win, at("off", 48 + c0, 48 + c1))
+
+        def add(i, c0, c1):
             tile, first = ("za", 0) if c0 < ca else ("zb", ca)
             out, offs, b = at(tile, 16 * (c0 - first), 16 * (c1 - first)), at("off", c0, c1), at("opb", 16 * c0, 16 * c1)
-            run("v", lambda: g.vector.tensor_tensor(out[0], ind(win, offs), b[0], Op.add), [win, offs, b], [out])
+            run("ga%d%s" % (i, tag), "v", lambda: g.vector.tensor_tensor(out[0], ind(win, offs), b[0], Op.add), [win, offs, b], [out])
+        for i, (c0, c1) in enumerate(cuts):
+            add(i, c0, c1)
             if c1 == ca:
-                quant("za", MINC * t, at("za"))
-                send(t, 2 * t, "za", MINC * t, la_, NA)
-        quant("zb", 0, at("zb"))
+                quant("qza" + tag, "za", MINC * t, at("za"))
+                send("sndA" + tag, t, 2 * t, "za", MINC * t, la_, NA)
+        quant("qzb" + tag, "zb", 0, at("zb", 0, 4 * WB))
         if t == 0:
-            act(at("cand", 0, ROUNDS * 2 * A, 2), at("cnt"), Fn.Identity, bias=float(C))
+            unit(1)
+            move("slot" + tag, "s", slot(0), slot(1))
         else:
-            act(slot(base), slot(t - 1, 2), Fn.Copy, offs=at("lsh", LI, LS))
-        layer("zb", 0, "hb", NB, 0, WB)
-        quant("hb", WB * t, at("hb"))
-        send(t, 2 * t + 1, "hb", WB * t, lb_, NB)
+            move("slot" + tag, "s", slot(base), slot(t - 1, 2), at("lsh", LI, LS))
+        layer("B" + tag, "zb", 0, "hb", NB, 0, WB)
+        quant("qhb" + tag, "hb", A * t, at("hb", 0, 4 * WB))
+        send("sndB" + tag, t, 2 * t + 1, "hb", A * t, lb_, NB)
 
+        plus("cnew" + tag, "s", at("cand", 2 * A * t, 2 * A * (t + 1), 2), at("cnt", 0, A), float(new))
         if t == 0:
-            act(at("c32"), at("zero", 0, 32), Fn.Identity, bias=col("cf", 3))
-            act(at("ids", 0, LS - LI), at("c16"), Fn.Identity, bias=col("cf", 2))
-            copy(at("lu", LD, LA), at("lst", LD, LA))
-            quant("l", 0, at("zero"))
-            quant("u", 0, at("ut"))
-            copy(at("upick", 0, 8), at("c16", 0, 8))
-            ts(at("upick", 8, 16), at("c32", 0, 8), 16.0, Op.mult)
-            act(at("ids", LS - LI), at("ids", 0, 8), Fn.Identity, scale=4.0, bias=3.0)
-        act(at("cand", 2 * A * t + 1, 2 * A * (t + 1), 2), slot(base), Fn.Copy, offs=at("lu", LD + 12 * t, LD + 12 * t + 12))
+            load("Lv", "y", at("vt"), T.v[:], after=[at("ql", lb_, lb_ + 1)])
+            move("sgn0", "s", at("sgn", 0, 2 * A, 2), at("zero", 0, A))
+            copy("lud", at("lu", LD, LI), at("lst", LD, LI))
+            quant("ql0", "l", 0, at("zero"))
+            quant("qu", "u", 0, at("ut"))
+            ts("up0", at("upick", 0, 8), at("k8"), 16.0, Op.mult)
+            ts("up1", at("upick", 8, 16), at("zero", 0, 8), col("cf", 3), Op.add, 16.0, Op.mult)
+            ts("ids0", at("ids", 0, LS - LI), at("cnt", 0, LS - LI), 16.0, Op.mult, col("cf", 2), Op.add)
+            ts("ids1", at("ids", LS - LI), at("ids", 0, 8), 4.0, Op.mult, 3.0, Op.add)
+        move("cold" + tag, "s", at("cand", 2 * A * t + 1, 2 * A * (t + 1), 2), slot(base), at("lu", LD + 12 * t, LD + 12 * t + 12))
         if t == 0:
-            run("v", lambda: g.vector.tensor_copy(T.qp[:, 0:256].bitcast(dt.uint32),
-                                                  T.qu[:, 0:128].bitcast(dt.uint32).indirect(T.upick[:, 0:16])),
+            run("pkq", "v", lambda: g.vector.tensor_copy(T.qp[:, 0:256].bitcast(dt.uint32),
+                                                         T.qu[:, 0:128].bitcast(dt.uint32).indirect(T.upick[:, 0:16])),
                 [at("qu"), at("upick")], [at("qp")])
-            act(at("sp", 0, 256), at("su", 0, 128), Fn.Copy, offs=at("upick", 0, 16))
-            for b in range(4):
+            act("pks", at("sp", 0, 256), at("su", 0, 128), Fn.Copy, offs=at("upick", 0, 16))
+            for b in (0, 2, 1, 3):
                 a = 516 * (b % 2) + 2 - 2 * (b // 2)
-                quant("e", 128 * b, at("unit", a, a + 512))
-            ts(at("tie", 0, 32), at("c32"), 0.125, Op.mult)
-            ts(col("tie", 32), col("cf", 4), 0.125, Op.mult)
-            ts(at("lf", LA, LI), at("lst", LA, LI), HALF + 0.25, Op.add, 1.0 / HALF, Op.mult)
-            ts(at("lf", LI, LE), at("ids"), HALF + 0.25, Op.add, 1.0 / HALF, Op.mult)
+                quant("qe%d" % b, "e", 128 * b, at("unit", a, a + 512))
+            ts("tie0", col("tie", 64), col("cf", 4), -2.0, Op.mult, col("cf", 3), Op.add)
+            ts("tie1", at("tie", 32, 64), at("cnt", 0, 32), 16.0, Op.is_ge, col("tie", 64), Op.subtract)
+            ts("tie2", at("tie", 0, 32), at("tie", 32, 64), -0.125, Op.mult)
+            ts("lf0", at("lf", LA + 12, LD), at("lst", LA + 12, LD), HALF + 0.25, Op.add, 1.0 / HALF, Op.mult)
+            ts("lf1", at("lf", LI, LE), at("ids"), HALF + 0.25, Op.add, 1.0 / HALF, Op.mult)
         if t == 1:
-            act(slot(3), slot(2), Fn.Copy)
-            quant("v", 0, at("vt"))
+            move("slot3", "s", slot(3), slot(2))
+            quant("qv", "v", 0, at("vt"))
         if t == 2:
-            scan(at("sel", 0, C), at("cpat"), slot(3), Op.add, Op.max)
+            scan("selrb", at("sel", 0, C), at("cpat"), slot(3), Op.add, Op.max)
 
-        def scores(part, bank, j0, n, skip):
+        def scores(r, part, bank, j0, n, skip):
             p = 512 * bank + skip
-            act(at("sgn", 2 * j0 + 1, 2 * (j0 + n), 2), at("ps", p, p + n), Fn.Sign, bias=at("tiny"), acc=col("acc", part))
-            act(at("junk", 0, n), at("ps", p + 512, p + 512 + n), Fn.Sign, bias=at("tiny"), acc=col("acc", 2 + part))
+            act("so" + r + tag, at("sgn", 2 * j0 + 1, 2 * (j0 + n), 2), at("ps", p, p + n), Fn.Sign, bias=at("tiny"), acc=col("acc", part))
+            act("sm" + r + tag, at("junk", j0, j0 + n), at("ps", p + 512, p + 512 + n), Fn.Sign, bias=at("tiny"), acc=col("acc", 2 + part))
 
-        def choose(j0, n):
-            scan(at("nv", 2 * j0, 2 * (j0 + n)), at("sgn", 2 * j0, 2 * (j0 + n)),
+        def choose(r, j0, n):
+            scan("ch" + r + tag, at("nv", 2 * j0, 2 * (j0 + n)), at("sgn", 2 * j0, 2 * (j0 + n)),
                  at("cand", 2 * (A * t + j0), 2 * (A * t + j0 + n)), Op.mult, Op.max)
 
-        def commit(j0, n):
+        def commit(r, j0, n):
             c = LD + 12 * t + j0 // 16
-            scatter(slot(base), at("lu", c, c + n // 16), at("nv", 2 * j0 + 1, 2 * (j0 + n), 2))
+            w, offs, in_ = slot(base), at("lu", c, c + n // 16), at("nv", 2 * j0 + 1, 2 * (j0 + n), 2)
+            run("cm" + r + tag, "v", lambda: g.vector.tensor_copy(ind(w, offs), in_[0]), [in_, offs, w], [w])
 
-        def unpack(b, q, j0, n, skip):
-            move(q, at("fil", 4 * (new + j0) + b, 4 * (new + j0 + n), 4), at("ps", 512 * b + skip, 512 * b + skip + n))
+        def unpack(r, b, q, j0, n, skip):
+            move("un%d%s%s" % (b, r, tag), q, at("fil", 4 * (new + j0) + b, 4 * (new + j0 + n), 4),
+                 at("ps", 512 * b + skip, 512 * b + skip + n))
 
-        own = col("tie", 32)
-        if NA:
-            layer("l", la_ + NA - MINC, "ha", NA, MINC - NA, MINC)
-            quant("ga", 0, at("ha"))
-            mm(4, "p", 0, "ga", 0)
-            mm(0, "e", 0, "ga", 0)
-            mm(5, "p", 128, "ga", 0)
-            for b in (2, 1, 3):
-                mm(b, "e", 128 * b, "ga", 0)
-            unpack(0, "v", 0, NA, 0)
-            scores(0, 4, 0, NA, 0)
-            choose(0, NA)
-            unpack(1, "v", 0, NA, 0)
-            unpack(2, "s", 0, NA, 0)
-            commit(0, NA)
-            unpack(3, "s", 0, NA, 0)
-            act(col("acc", 4), own, Fn.Identity, bias=col("acc", 0))
-            own = col("acc", 4)
+        layer("A" + tag, "l", la_ + NA - MINC, "ha", NA, MINC - NA, MINC)
+        quant("qga" + tag, "ga", 0, at("ha"))
+        mm("moA" + tag, 4, "p", 0, "ga", 0)
+        mm("me0A" + tag, 0, "e", 0, "ga", 0)
+        mm("mmA" + tag, 5, "p", 128, "ga", 0)
+        for b in (2, 1, 3):
+            mm("me%dA%s" % (b, tag), b, "e", 128 * b, "ga", 0)
+        unpack("A", 0, "v", 0, NA, 0)
+        scores("A", 0, 4, 0, NA, 0)
+        choose("A", 0, NA)
+        plus("kea" + tag, "s", at("tie", 32, 64), at("tie", 0, 32), col("acc", 2))
+        unpack("A", 2, "s", 0, NA, 0)
+        commit("A", 0, NA)
+        unpack("A", 1, "s", 0, NA, 0)
+        unpack("A", 3, "s", 0, NA, 0)
 
         xa, skip = lb_ + NB - WB, WB - NB
-        mm(6, "p", 0, "l", xa, WB)
-        mm(0, "e", 0, "l", xa, WB)
-        mm(7, "p", 128, "l", xa, WB)
-        for b in (1, 2, 3):
-            mm(b, "e", 128 * b, "l", xa, WB)
-        unpack(0, "v", NA, NB, skip)
-        scores(1, 6, NA, NB, skip)
-        choose(NA, NB)
-        act(col("acc", 5), own, Fn.Identity, bias=col("acc", 1))
-        if NA:
-            ts(at("key", 0, 32), at("tie", 0, 32), col("acc", 2), Op.add, col("acc", 3), Op.add)
-        else:
-            ts(at("key", 0, 32), at("tie", 0, 32), col("acc", 3), Op.add)
-        run("v", lambda: g.vector.transpose(T.key[:, 32:64], T.key[:, 0:32]), [at("key", 0, 32)], [at("key", 32, 64)])
-        unpack(1, "s", NA, NB, skip)
-        commit(NA, NB)
-        act(at("cmp"), at("key", 32, 40), Fn.Sign, scale=-1.0, bias=col("acc", 5), acc=col("acc", 6))
+        mm("moB" + tag, 6, "p", 0, "l", xa, WB)
+        mm("mmB" + tag, 7, "p", 128, "l", xa, WB)
+        for b in (0, 2, 1, 3):
+            mm("me%dB%s" % (b, tag), b, "e", 128 * b, "l", xa, WB)
+        scores("B", 1, 6, NA, NB, skip)
+        choose("B", NA, NB)
+        plus("own" + tag, "s", col("acc", 5), col("acc", 0), col("acc", 1))
+        plus("key" + tag, "s", at("key", 0, 32), at("tie", 32, 64), col("acc", 3))
+        run("tr" + tag, "v", lambda: g.vector.transpose(T.key[:, 32:64], T.key[:, 0:32]), [at("key", 0, 32)], [at("key", 32, 64)])
+        unpack("B", 0, "s", NA, NB, skip)
+        commit("B", NA, NB)
+        act("cmp" + tag, at("cmp"), at("key", 32, 40), Fn.Sign, scale=-1.0, bias=col("acc", 5), acc=col("acc", 6))
         side = -1.0 if t == 0 else 1.0
-        act(at("keep"), col("acc", 6), Fn.Sign, scale=side, bias=4.0 * side)
-        unpack(2, "s", NA, NB, skip)
+        act("keep" + tag, at("keep"), col("acc", 6), Fn.Sign, scale=side, bias=4.0 * side)
+        unpack("B", 2, "s", NA, NB, skip)
         if t < ROUNDS - 1:
-            a = LA + 12 * (t + 1)
-            ts(at("lsh", a, LS), at("lf", a, LS), at("keep"), Op.add, HALF, Op.mult)
+            a = 12 * (t + 1)
+            ts("lsh" + tag, at("lsh", LA + a, LB + a + 12), at("lf", LA + a, LB + a + 12), at("keep"), Op.add, HALF, Op.mult)
+            unpack("B", 1, "v", NA, NB, skip)
+            unpack("B", 3, "s", NA, NB, skip)
             places(slot(t, 2), "lsh", t + 1)
-            unpack(3, "s", NA, NB, skip)
-            offsets()
+            ts("lsi" + tag, at("lsh", LI, LS), at("lf", LI, LS), at("keep"), Op.add, HALF, Op.mult)
         else:
-            ts(at("lsh", LI, LE), at("lf", LI, LE), at("keep"), Op.add, HALF, Op.mult)
-            unpack(3, "s", NA, NB, skip)
-            scan(at("sel", C, 2 * C), at("cpat"), slot(4), Op.add, Op.max)
-            ts(at("off"), at("sel"), 4.0, Op.mult, col("addc", 1), Op.add, offs=at("lsh", LS, LS + 7))
-            act(at("omr"), slot(3, 2), Fn.Copy, offs=at("lsh", LI, LS))
+            scan("selA", at("sel", C, C + T1), at("cpat", 0, T1), at("maps", 4 * C, 4 * C + T1), Op.add, Op.max)
+            ts("lsh" + tag, at("lsh", LI, LE), at("lf", LI, LE), at("keep"), Op.add, HALF, Op.mult)
+            unpack("B", 1, "s", NA, NB, skip)
+            unpack("B", 3, "s", NA, NB, skip)
+            ts("ofA", at("off", 0, T1 // 4), at("sel", 0, C + T1), 4.0, Op.mult, col("addc", 1), Op.add, offs=at("lsh", LS, LS + T1 // 64))
+            scan("selB", at("sel", C + T1, 2 * C), at("cpat", 0, C - T1), at("maps", 4 * C + T1, 5 * C), Op.add, Op.max)
+            ts("ofB", at("off", T1 // 4), at("sel"), 4.0, Op.mult, col("addc", 1), Op.add, offs=at("lsh", LS + T1 // 64, LS + 7))
 
-    store("y", T.om[:], at("omr", rows=slice(0, 128, 16)))
+    for t in range(ROUNDS):
+        one_round(t)
+
     win = at("fil")
-    runs = len(TCUT) - 1
-
-    def result(k, q):
-        a, b = TCUT[k], TCUT[k + 1]
-        move(q, at("ysb", a, b), at("ps", 512 * k, 512 * k + b - a))
-        store("s" if q == "s" else "y", T.y[:, a:b], at("ysb", a, b))
-
-    for k in range(runs):
-        c0, c1 = TCUT[k] // 4, TCUT[k + 1] // 4
-        cm = c0 + TSHARE[k]
-        act(at("tt", 16 * cm, 16 * c1), win, Fn.Copy, offs=at("off", cm, c1))
-        copy(at("tt", 16 * c0, 16 * cm), win, offs=at("off", c0, cm))
-        if k:
-            result(k - 1, "s")
-        a, b = TCUT[k], TCUT[k + 1]
-        quant("t", a, at("tt", 4 * a, 4 * b))
-        store("y", T.oc[:, 4 * a:4 * b], at("qt", a, b), codes=True)
-        mm(k, "v", 0, "t", a, b - a)
+    k = 0
+    for i, (c0, c1) in enumerate(zip(TG[:-1], TG[1:])):
+        move("gt%d" % i, "sv"[i % 2], at("tt", 16 * c0, 16 * c1), win, at("off", c0, c1))
+        if 4 * c1 == TCUT[k + 1]:
+            a, b = TCUT[k], TCUT[k + 1]
+            quant("qt%d" % k, "t", a, at("tt", 4 * a, 4 * b))
+            mm("my%d" % k, k, "v", 0, "t", a, b - a)
+            move("ey%d" % k, "s", at("ysb", a, b), at("ps", 512 * k, 512 * k + b - a))
+            k += 1
+    for k, (a, b) in enumerate(zip(CCUT[:-1], CCUT[1:])):
+        store("Sc%d" % k, "y", T.oc[:, 4 * a:4 * b], at("qt", a, b), codes=True)
+    for k, (a, b) in enumerate(zip(YCUT[:-1], YCUT[1:])):
+        store("Sy%d" % k, "y", T.y[:, a:b], at("ysb", a, b))
     for i in range(4):
-        store("s" if i > 0 else "y", T.osc[4 * i:4 * i + 4, :], at("st", rows=slice(32 * i, 32 * i + 4)))
-    result(runs - 1, "v")
+        store("Ss%d" % i, "y", T.osc[4 * i:4 * i + 4, :], at("st", rows=slice(32 * i, 32 * i + 4)))
+    for h in range(2):
+        move("om%d" % h, "s", at("omr", 224 * h, 224 * h + 224), slot(3, 2), at("lsh", LI + 14 * h, LI + 14 * h + 14))
+    store("So", "y", T.om[:], at("omr", rows=slice(0, 128, 16)))
+
+    for name in ([n.strip("+-") for n in ORDER.split()] or list(steps)):
+        steps[name]()
     for sem, n in total.items():
         g.wait_ge(T.sem[sem], n)

@@ -1,55 +1,55 @@
-from concourse.mybir import dt, AluOpType as Op, ActivationFunctionType as Fn
+from concourse.mybir import dt, AluOpType as Op, ActivationFunctionType as Fn, AxisListType as Ax
 
 C, A, ROUNDS = 448, 192, 3
 NAS = [64, 96, 96]
 MINC = 128
-RAMP, DROP = 2048.0, 65536.0
+BASE = 4096
 TINY = 2.0 ** -126
 HALF = C / 2
-ZCUT = [[0, 8, 16, 32, 48], [0, 12, 24, 36, 48], [0, 12, 24, 36, 48]]
-TCUT = [0, 160, 320, 448]
-TG = [0, 32, 40, 66, 80, 100, 112]
-CCUT = [0, 160, 320, 448]
-YCUT = [0, 160, 320, 448]
+ACUT = [[0, 4, 16], [0, 6, 24], [0, 6, 24]]
+BCUT = [[0, 16, 32], [0, 12, 24], [0, 12, 24]]
+TCUT = [0, 128, 288, 448]
+TG = [0, 20, 32, 56, 72, 96, 112]
+CCUT = [0, 128, 288, 448]
+YCUT = [0, 128, 288, 448]
+GP = "slot3"
+SPLIT = "gaB0_0 gaB1_1 gaB0_2"
 T1 = 128
-WIDE = [False, False, False]
+LANES = "co ee cc cc cc cc"
 LAND = MINC + ROUNDS * A
-F32, BF, I32, U16, Q4, U8 = "float32", "bfloat16", "int32", "uint16", "float8_e4m3fn_x4", "uint8"
-LM, LA, LB, LD, LI, LS, LE = 0, 28, 64, 100, 136, 164, 172
+PRE = 8 * A
+F32, BF, I32, U16, Q4, U8, H16 = "float32", "bfloat16", "int32", "uint16", "float8_e4m3fn_x4", "uint8", "float16"
+LM, LA, LI, LS, LB, LD, LU, LK, LE = 0, 28, 64, 92, 100, 136, 172, 180, 208
 ORDER = """
-pcol za0 Lm La Lb Lx Lwc k8 tiny Lu ci1 Lws Ld ci0 cnt zero cfa ci3 c4a adc0 c4b ones cpat2+ cpat0+ lum ha0 cpat3+ unit0 adc1 map1 map0 lul cpat1+ ci4 ci2 lkb0_0- lkb1_0+ cfb lka0_0+ scb_0 unit1 lka1_0+ zb0 ofb_0 sca_0 hb0 ofa_0 up1 gb0_0+ gb1_0+ ga0_0 gb2_0+ ga1_0 up0 qza_0 gb3_0+ ga2_0 sndA_0 sgn0+ ga3_0 cnew_0+ slot_0+ ids0 tie0 qzb_0 ids1 mw3B_0 ql0 mw2B_0 tie1 ev3B_0+ qu mw0B_0 mw1B_0 ev2B_0- ev1B_0+ lud tie2 qe0 ev0B_0+ lf1 pks qhb_0 qe2 sndB_0 pkq mw2A_0 mw0A_0 ev2A_0+ mw1A_0 ev0A_0+ mw3A_0 ev1A_0+ ev3A_0- cold_0+ qga_0 qe3 moA_0 qe1 mmA_0 soA_0 me0A_0 lf0 smA_0 me2A_0 un0A_0- me3A_0 Lv un2A_0+ chA_0 moB_0 kea_0+ mmB_0 un3A_0- soB_0 me0B_0 cmA_0 me2B_0 smB_0 me1A_0 chB_0 me3B_0 un2B_0+ key_0+ un1A_0- un0B_0+ own_0- me1B_0 tr_0 cmB_0 cmp_0 un1B_0+ keep_0 un3B_0+ lsh_0
-lkb1_1+ lkb0_1- lsi_0 lka1_1+ scb_1 lka0_1+ ofb_1 gb0_1+ sca_1 ofa_1 gb1_1+ ga0_1 gb2_1+ ga1_1 gb3_1+ qza_1 ga2_1 sndA_1 slot_1+ ga3_1 qzb_1 slot3+ mw0B_1 mw2B_1 ev0B_1- mw3B_1 ev2B_1- mw1B_1 ev3B_1+ ev1B_1- qhb_1 sndB_1 mw0A_1 mw2A_1 ev0A_1+ mw3A_1 ev2A_1- mw1A_1 ev3A_1+ ev1A_1- cold_1+ qga_1 cnew_1- moA_1 me0A_1 soA_1 qv me1A_1 un0A_1- mmA_1 un1A_1+ me3A_1 chA_1 me2A_1 smA_1 un3A_1- un2A_1+ kea_1- moB_1 cmA_1 mmB_1 soB_1 me0B_1 me1B_1 smB_1 me2B_1 chB_1 me3B_1 key_1+ own_1- un2B_1+ tr_1 cmB_1 cmp_1 keep_1 un3B_1+ lsh_1 un0B_1+
-lkb0_2- lkb1_2+ un1B_1- lka0_2+ scb_2 lka1_2+ ofb_2 sca_2 gb0_2+ ofa_2 lsi_1 gb1_2+ ga0_2 gb2_2+ ga1_2 gb3_2+ qza_2 ga2_2 sndA_2 slot_2+ ga3_2 qzb_2 cnew_2+ selrb mw2B_2 mw0B_2 ev2B_2+ mw3B_2 mw1B_2 ev0B_2+ ev1B_2- ev3B_2+ qhb_2 sndB_2 mw1A_2 mw3A_2 ev1A_2- mw2A_2 ev3A_2+ mw0A_2 ev2A_2+ ev0A_2- cold_2+ qga_2 moA_2 me0A_2 soA_2 mmA_2 un0A_2- me2A_2 smA_2 chA_2 me3A_2 me1A_2 kea_2+ un3A_2- un2A_2+ cmA_2 moB_2 mmB_2 soB_2 me3B_2 un1A_2- me0B_2 smB_2 me2B_2 chB_2 own_2+ me1B_2 key_2+ un0B_2+ tr_2 cmB_2 cmp_2 keep_2 un1B_2+ lsh_2 un2B_2+
-selA un3B_2+ ofA selB gt0+ ofB gt1- gt2+ qt0 gt3- Sc0- my0 ey0- gt4+ qt1 Sy0- gt5- Sc1- my1 om0+ qt2 ey1- my2 Sc2- Ss0+ Ss1- Ss2+ Ss3- ey2+ om1- Sy1- Sy2- So+
+La- Lm+ p16 ones Lb- Lx+ i16 Lwc- Lws+ Ld- cnt Lu- cir cia upick cf4 cib tiny c4 sgn0 cpat1+ cpat3+ cpat0+ cf chalf- cpat2- ids0 tie0 cnew_1+ unit tie1+ lum map0- map1+ lub cadd cmul lkaA_0+ lkbA_0- lkaB_0- lkbB_0+ scA_0 cnew_2+ ids1 ofA_0 scB_0 gbA1_0+ gbA0_0- ofB_0 gaA0_0 gbB1_0+ gaA1_0 gsB0_0+ qza_0 qe1 gbB0_0+ sndA_0 gaB1_0 cnew_0+ slot_0+ gaB0_0 lud qzb_0 cold_0+ lf mw1B_0 qu mw2B_0 ev1B_0+ mw3B_0 ev2B_0- mw0B_0 ev3B_0+ pks+ ev0B_0- qhb_0 qe3 sndB_0 qe0 mw3A_0 pkq mw2A_0 ev3A_0+ mw0A_0 ev2A_0- mw1A_0 ev0A_0+ ev1A_0- qga_0 qe2 moA_0 mmA_0 soA_0 Lv- chA_0 moB_0 smA_0 kea_0- cmA_0 mmB_0 soB_0 me3A_0 smB_0 chB_0 me0A_0 own_0+ key_0+ un3A_0+ tr_0 me2A_0 cmB_0 un0A_0+ cmp_0 me1A_0 un2A_0+ keep_0 me3B_0 lsh_0 me0B_0 un3B_0+ un1A_0- me2B_0 un0B_0+
+lkaA_1- lkbA_1+ me1B_0 lkaB_1- lkbB_1+ scA_1 un2B_0+ ofA_1 scB_1 un1B_0+ gbA1_1+ gbA0_1- ofB_1 gaA0_1 gbB0_1+ gaA1_1 gbB1_1+ gsB1_1+ qza_1 gaB0_1 sndA_1 slot_1+ gaB1_1 qzb_1 mw0B_1 mw1B_1 ev0B_1+ mw3B_1 ev1B_1- mw2B_1 ev3B_1+ cold_1+ ev2B_1- mw0A_1 qhb_1 mw1A_1 sndB_1 slot3 ev0A_1+ mw3A_1 ev1A_1- mw2A_1 ev3A_1+ ev2A_1- qga_1 moA_1 mmA_1 soA_1 chA_1 me2A_1 smA_1 me1A_1 un2A_1+ kea_1+ me3A_1 un1A_1- cmA_1 moB_1 un3A_1+ mmB_1 soB_1 me0A_1 smB_1 chB_1 me3B_1 un0A_1+ key_1- own_1- tr_1 cmB_1 me1B_1 un3B_1+ cmp_1 me2B_1 keep_1 un1B_1+ lsh_1 me0B_1 un2B_1+
+lkaA_2- lkbA_2+ lkbB_2- lkaB_2+ scA_2 un0B_1+ ofA_2 scB_2 gbA1_2+ gbA0_2- ofB_2 gaA0_2 gbB1_2+ gaA1_2 gbB0_2+ gsB0_2+ qza_2 slot_2+ gaB1_2 sndA_2 gaB0_2 qzb_2 qv mw3B_2 mw1B_2 ev3B_2+ mw2B_2 ev1B_2- mw0B_2 ev2B_2+ cold_2+ ev0B_2- mw3A_2 qhb_2 mw1A_2 sndB_2 ev3A_2+ mw2A_2 ev1A_2- mw0A_2 ev2A_2+ ev0A_2- qga_2 selrb moA_2 mmA_2 soA_2 me3A_2 smA_2 chA_2 me2A_2 un3A_2+ kea_2+ me0A_2 un2A_2- cmA_2 moB_2 un0A_2+ mmB_2 soB_2 me1A_2 smB_2 chB_2 me2B_2 un1A_2+ key_2- own_2- tr_2 cmB_2 me0B_2 un2B_2+ cmp_2 me3B_2 keep_2 un0B_2+ lsh_2 me1B_2
+selA un3B_2+ ofT0 un1B_2+ selB gt0+ gt1- ofT1 qt0 gt3+ gt2- Sc0- my0 ey0+ gt4+ Sy0- qt1 gt5- my1 Sc1- ey1+ qt2 om1+ Sy1- om0- Ss0- my2 Sc2- Ss2+ ey2+ So- Ss3- Sy2+ Ss1+
 """
-ENG = {n[:-1]: "s" if n[-1] == "+" else "vy"[n[0] == "S"] for n in ORDER.split() if n[-1] in "+-"}
+ENG = {n[:-1]: "s" if n[-1] == "+" else "vy"[n[0] in "SL"] for n in ORDER.split() if n[-1] in "+-"}
 
 SCRATCH = {
-    "lst": ("sbuf", [128, LI], I32), "lu": ("sbuf", [128, LI], U16), "ids": ("sbuf", [128, LE - LI], F32),
-    "lf": ("sbuf", [128, LE], F32), "lsh": ("sbuf", [128, LE], U16),
-    "fil": ("sbuf", [128, 4096], BF), "maps": ("sbuf", [128, 5 * C], F32),
-    "cnt": ("sbuf", [128, C], F32), "pcol": ("sbuf", [128, 1], I32), "k8": ("sbuf", [128, 8], F32),
-    "ci": ("sbuf", [128, 8], I32), "cf": ("sbuf", [128, 8], F32),
-    "c4": ("sbuf", [128, 8], F32), "addc": ("sbuf", [128, 2], F32), "tiny": ("sbuf", [128, 1], F32),
-    "cpat": ("sbuf", [128, C], F32), "upick": ("sbuf", [128, 16], U16),
-    "tie": ("sbuf", [128, 68], F32),
-    "zero": ("sbuf", [128, 512], BF), "ones": ("sbuf", [128, 516], BF), "unit": ("sbuf", [128, 1032], BF),
+    "lst": ("sbuf", [128, LE], I32), "lu": ("sbuf", [128, LE], U16),
+    "lf": ("sbuf", [128, LD], F32), "lsh": ("sbuf", [128, LD], U16),
+    "fil": ("sbuf", [128, PRE + 4096], BF), "maps": ("sbuf", [128, 5 * C], F32),
+    "cnt": ("sbuf", [128, C], F32), "p16": ("sbuf", [128, 8], I32), "c4": ("sbuf", [128, 4], F32),
+    "ci": ("sbuf", [128, 4], I32), "cf": ("sbuf", [128, 12], F32), "tiny": ("sbuf", [128, 1], F32),
+    "cpat": ("sbuf", [128, C], H16), "tie": ("sbuf", [128, 96], F32),
+    "ones": ("sbuf", [128, 516], BF), "unit": ("sbuf", [128, 516], BF),
     "qe": ("sbuf", [128, 512], Q4), "se": ("sbuf", [128, 512], U8),
     "qw": ("sbuf", [128, 512], Q4), "sw": ("sbuf", [128, 512], U8),
     "ut": ("sbuf", [128, 512], BF), "vt": ("sbuf", [128, 512], BF),
     "qu": ("sbuf", [128, 128], Q4), "su": ("sbuf", [128, 128], U8),
     "qp": ("sbuf", [128, 256], Q4), "sp": ("sbuf", [128, 256], U8),
     "qv": ("sbuf", [128, 128], Q4), "sv": ("sbuf", [128, 128], U8),
-    "row": ("sbuf", [128, 2 * A], F32), "scn": ("sbuf", [128, 2 * A], F32), "off": ("sbuf", [128, 112], U16),
-    "opb": ("sbuf", [128, 4 * A], BF),
-    "za": ("sbuf", [128, 4 * MINC], BF), "zb": ("sbuf", [128, 4 * A], BF),
-    "ha": ("sbuf", [128, 4 * MINC], BF), "hb": ("sbuf", [128, 4 * A], BF),
+    "row": ("sbuf", [128, 2 * A + 32], H16), "scn": ("sbuf", [128, 2 * A + 32], H16), "off": ("sbuf", [128, 112], U16),
+    "opb": ("sbuf", [128, 4 * A], BF), "opa": ("sbuf", [128, 4 * A], BF),
     "qza": ("sbuf", [128, ROUNDS * MINC], Q4), "sza": ("sbuf", [128, ROUNDS * MINC], U8),
     "qhb": ("sbuf", [128, ROUNDS * A], Q4), "shb": ("sbuf", [128, ROUNDS * A], U8),
     "qzb": ("sbuf", [128, A], Q4), "szb": ("sbuf", [128, A], U8),
     "qga": ("sbuf", [128, MINC], Q4), "sga": ("sbuf", [128, MINC], U8),
     "ql": ("sbuf", [128, LAND], Q4), "sl": ("sbuf", [128, LAND], U8),
-    "sgn": ("sbuf", [128, 2 * A], F32), "cand": ("sbuf", [128, ROUNDS * 2 * A], F32), "nv": ("sbuf", [128, 2 * A], F32),
+    "sgn": ("sbuf", [128, 2 * A], BF), "cand": ("sbuf", [128, ROUNDS * 2 * A], H16), "nv": ("sbuf", [128, 2 * A], H16),
     "junk": ("sbuf", [128, A], BF), "acc": ("sbuf", [128, 8], F32), "key": ("sbuf", [128, 64], F32),
     "cmp": ("sbuf", [128, 8], F32), "keep": ("sbuf", [128, 1], F32),
     "sel": ("sbuf", [128, 2 * C], F32), "omr": ("sbuf", [128, C], F32),
@@ -147,22 +147,25 @@ def rank_program(g, core, T, topo):
             [in_] + [s for s in (bias, scale, offs) if isap(s)], [out] + ([acc] if acc else []))
 
     def move(nm, q, out, in_, offs=None):
-        if ENG.get(nm, q) == "v":
+        if nm in GP.split():
+            n = out[0].shape[1]
+            run(nm, "g", lambda: g.affine_select(out[0], in_[0], [[0, n]], Op.is_ge, 0.0, 0, 0), [in_], [out])
+        elif ENG.get(nm, q) == "v":
             copy(nm, out, in_, offs)
         else:
             act(nm, out, in_, Fn.Copy, offs=offs)
 
-    def plus(nm, q, out, in_, s):
+    def affine(nm, q, out, in_, scale, bias, offs=None):
         if ENG.get(nm, q) == "v":
-            ts(nm, out, in_, s, Op.add)
+            ts(nm, out, in_, scale, Op.mult, bias, Op.add, offs=offs)
         else:
-            act(nm, out, in_, Fn.Identity, bias=s)
+            act(nm, out, in_, Fn.Identity, bias=bias, scale=scale, offs=offs)
 
     def fill(nm, out, value):
         run(nm, "v", lambda: g.vector.memset(out[0], value), [], [out])
 
-    def scan(nm, out, d0, d1, op0, op1):
-        run(nm, "v", lambda: g.vector.tensor_tensor_scan(out[0], d0[0], d1[0], 0.0, op0, op1), [d0, d1], [out])
+    def scan(nm, out, d0, d1):
+        run(nm, "v", lambda: g.vector.tensor_tensor_scan(out[0], d0[0], d1[0], 0.0, Op.mult, Op.max), [d0, d1], [out])
 
     def quant(nm, name, a, tile):
         n = tile[0].shape[1] // 4
@@ -177,6 +180,7 @@ def rank_program(g, core, T, topo):
 
     def load(nm, q, out, src, codes=False, after=()):
         dst = out[0].bitcast(dt.uint8) if codes else out[0]
+        q = ENG.get(nm, q)
         run(nm, q, lambda: queue[q].dma_start(dst, src), list(after), [out], dma=True)
 
     def store(nm, q, dst, in_, codes=False):
@@ -184,9 +188,9 @@ def rank_program(g, core, T, topo):
         q = ENG.get(nm, q)
         run(nm, q, lambda: queue[q].dma_start(dst, src), [in_], [], dma=True)
 
-    def iota(nm, out, pattern, cm, small=True):
-        kw = {"allow_small_or_imprecise_dtypes": True} if small else {}
-        run(nm, "g", lambda: g.iota(out[0], pattern, 0, cm, **kw), [], [out])
+    def iota(nm, out, pattern, base, cm, whole=False):
+        kw = {} if whole else {"allow_small_or_imprecise_dtypes": True}
+        run(nm, "g", lambda: g.iota(out[0], pattern, base, cm, **kw), [], [out])
 
     partners = [T.cores[rank ^ (1 << t)] for t in range(ROUNDS)]
     common = topo.mask(core, partners[0])
@@ -195,18 +199,20 @@ def rank_program(g, core, T, topo):
 
     def send(nm, t, k, name, a, land, n):
         rid, pid = topo.addr(partners[t], core)
-        mask = topo.mask(core, partners[t]) if WIDE[t] else common
-        lanes = bin(mask).count("1")
+        every = topo.mask(core, partners[t])
+        second = sum(1 << e for e in topo.engines(core, partners[t])[::2])
+        masks = [{"c": common, "o": every & ~common, "e": every, "s": second}[c] for c in LANES.split()[k]]
+        lanes = sum(bin(m).count("1") for m in masks)
         sem = "arr%d" % k
         src = [at("q" + name, a, a + n), at("s" + name, a, a + n)]
         dst = [at("ql", land, land + n), at("sl", land, land + n)]
 
         def emit():
             order("g", [s[1] for s in src], [])
-            g.remote_dma(dst[0][0].bitcast(dt.uint8), src[0][0].bitcast(dt.uint8), T.sem[sem], T.sem.sent, pid, rid, mask)
-            g.remote_dma(dst[1][0], src[1][0], T.sem[sem], T.sem.sent, pid, rid, mask)
-            total["sent"] = total.get("sent", 0) + 2 * lanes
-            note([], [d[1] for d in dst], sem, 2 * lanes, {})
+            g.remote_dma(dst[0][0].bitcast(dt.uint8), src[0][0].bitcast(dt.uint8), T.sem[sem], T.sem.sent, pid, rid, masks[0])
+            g.remote_dma(dst[1][0], src[1][0], T.sem[sem], T.sem.sent, pid, rid, masks[1])
+            total["sent"] = total.get("sent", 0) + lanes
+            note([], [d[1] for d in dst], sem, lanes, {})
         steps[nm] = emit
 
     def slot(k, n=1):
@@ -215,67 +221,66 @@ def rank_program(g, core, T, topo):
     def col(name, k):
         return at(name, k, k + 1)
 
+    def tile(a, n):
+        return at("fil", 4 * a, 4 * (a + n))
+
     load("Lm", "y", at("lst", LM, LA), T.m[:])
-    load("La", "s", at("lst", LA, LB), T.la[:])
+    load("La", "s", at("lst", LA, LI), T.la[:])
     load("Lb", "y", at("lst", LB, LD), T.lb[:])
-    load("Lx", "y", at("fil", 0, 4 * C), T.x[:])
+    load("Lx", "y", at("fil", PRE, PRE + 4 * C), T.x[:])
     load("Lwc", "y", at("qw"), T.wc[:], codes=True)
     load("Lws", "y", at("sw"), T.ws[:])
-    load("Ld", "y", at("lst", LD, LI), T.ld[:])
+    load("Ld", "y", at("lst", LD, LU), T.ld[:])
     load("Lu", "y", at("ut"), T.u[:])
 
-    iota("pcol", at("pcol"), [[0, 1]], 1, small=False)
-    iota("k8", at("k8"), [[1, 8]], 0)
-    iota("cnt", at("cnt"), [[1, C]], 0)
+    iota("p16", at("p16"), [[0, 8]], 0, 16, whole=True)
+    iota("cnt", at("cnt"), [[4, C]], BASE, 0)
+    iota("i16", at("lst", LK, LE), [[16, LE - LK]], 0, 0, whole=True)
+    iota("tie0", at("tie", 64, 96), [[-2, 2], [0, 16]], 1, 2)
     fill("tiny", at("tiny"), TINY)
-    fill("za0", at("za", 4 * min(NAS)), 0.0)
-    ts("ci0", col("ci", 0), at("pcol"), 15, Op.bitwise_and, 2, Op.logical_shift_right)
-    ts("ci1", col("ci", 1), at("pcol"), 3, Op.bitwise_and)
-    ts("ci2", col("ci", 2), at("pcol"), 15, Op.bitwise_and)
-    copy("cfa", at("cf", 0, 2), at("ci", 0, 2))
-    ts("ci3", col("ci", 3), at("pcol"), 7, Op.bitwise_and)
-    ts("c4a", at("c4", 0, 4), at("k8", 0, 4), col("cf", 0), Op.is_gt, RAMP + DROP, Op.mult)
-    ts("ci4", col("ci", 4), at("pcol"), 5, Op.logical_shift_right)
-    ts("c4b", at("c4", 4, 8), at("c4", 0, 4), -DROP, Op.add)
-    fill("zero", at("zero"), 0.0)
-    for k in range(4):
-        plus("cpat%d" % k, "s", at("cpat", k, C, 4), at("zero", 0, C // 4), col("c4", 4 + k))
     fill("ones", at("ones"), 1.0)
-    ts("adc0", col("addc", 0), col("cf", 0), 4 * RAMP, Op.mult, -12 * RAMP, Op.add)
-    copy("cfb", at("cf", 2, 5), at("ci", 2, 5))
-    ts("adc1", col("addc", 1), col("addc", 0), col("cf", 1), Op.add)
-    if A - max(NAS) < MINC:
-        fill("zb0", at("zb", 4 * (A - max(NAS)), 4 * MINC), 0.0)
-        fill("hb0", at("hb", 4 * (A - max(NAS)), 4 * MINC), 0.0)
-    fill("ha0", at("ha", 4 * min(NAS)), 0.0)
+    fill("sgn0", at("sgn"), 0.0)
+    ts("cir", col("ci", 0), col("p16", 0), 255, Op.bitwise_and, 4, Op.logical_shift_right)
+    ts("cia", col("ci", 1), col("p16", 0), 9, Op.logical_shift_right)
+    ts("cib", col("ci", 2), col("p16", 0), 63, Op.bitwise_and, 4, Op.logical_shift_right)
+    copy("cf", at("cf", 0, 2), at("ci", 0, 2))
+    ts("cf4", col("cf", 8), col("ci", 0), 4.0, Op.mult)
+    ts("cadd", col("cf", 2), col("ci", 2), -float(BASE), Op.add)
+    ts("c4", at("c4"), at("lst", LK, LK + 4), col("cf", 8), Op.is_gt, 2.0, Op.mult)
+    for k in range(4):
+        affine("cpat%d" % k, "s", at("cpat", k, C, 4), at("ones", 0, C // 4), col("c4", k), 0.0)
+    affine("chalf", "v", at("cf", 4, 8), at("c4"), -0.25, 1.0)
+    run("cmul", "v", lambda: g.vector.tensor_reduce(T.cf[:, 3:4], T.cf[:, 4:8], Ax.X, Op.mult), [at("cf", 4, 8)], [col("cf", 3)])
+    cmul, cadd = col("cf", 3), col("cf", 2)
+    run("unit", "g", lambda: g.affine_select(T.unit[:], T.ones[:], [[-1, 516]], Op.is_equal, 0.0, 3, 4), [at("ones")], [at("unit")])
 
-    def unit(i):
-        out = at("unit", 516 * i, 516 * (i + 1))
-        run("unit%d" % i, "g", lambda: g.affine_select(out[0], T.ones[:], [[-1, 516]], Op.is_equal, 0.0, 2 + i, 4),
-            [at("ones")], [out])
-    unit(0)
+    copy("lum", at("lu", LM, LA + 12), at("lst", LM, LA + 12))
+    move("map0", "v", at("maps", C, C + 224), at("cnt"), at("lu", LM, LM + 14))
+    move("map1", "s", at("maps", C + 224, 2 * C), at("cnt"), at("lu", LM + 14, LA))
+    copy("lub", at("lu", LB, LB + 12), at("lst", LB, LB + 12))
 
-    copy("lum", at("lu", LM, LA), at("lst", LM, LA))
-    copy("map0", at("maps", C, C + 192), at("cnt"), offs=at("lu", LM, LM + 12))
-    act("map1", at("maps", C + 192, 2 * C), at("cnt"), Fn.Copy, offs=at("lu", LM + 12, LA))
-    copy("lul", at("lu", LA, LB + 12), at("lst", LA, LB + 12))
+    def parts(t):
+        na = NAS[t] // 16
+        gap = 16 * (na % 2)
+        b2 = 32 * na + gap
+        return [(0, na, 0, 16 * na, 0), (na - na % 2, 12 - na + na % 2, b2, b2 + A - 16 * na + gap, gap)]
 
     def places(win, lists, t):
-        for o, l, r in (("b", LB, A), ("a", LA, 0)):
-            for h in range(2):
-                move("lk%s%d_%d" % (o, h, t), "v" if (o, h) == ("b", 0) else "s", at("row", r + 96 * h, r + 96 * h + 96), win,
-                     at(lists, l + 12 * t + 6 * h, l + 12 * t + 6 * h + 6))
-        for o, r in (("b", A), ("a", 0)):
-            scan("sc%s_%d" % (o, t), at("scn", r, r + A), at("cpat", 0, A), at("row", r, r + A), Op.add, Op.max)
-            ts("of%s_%d" % (o, t), at("off", r // 4, r // 4 + 48), at("scn", r + 3, r + A, 4), 4.0, Op.mult, col("addc", 1), Op.add)
+        for r, (c0, n, pb, pa, gap) in zip("AB", parts(t)):
+            for o, l, p in (("b", LB, pb), ("a", LA, pa)):
+                move("lk%s%s_%d" % (o, r, t), "v" if (o, r) == ("a", "A") else "s", at("row", p - gap, p - gap + 16 * n), win,
+                     at(lists, l + 12 * t + c0, l + 12 * t + c0 + n))
+            end = pa - gap + 16 * n
+            scan("sc%s_%d" % (r, t), at("scn", pb, end), at("cpat", 0, end - pb), at("row", pb, end))
+            ts("of%s_%d" % (r, t), at("off", pb // 4, end // 4), at("scn", pb + 3, end, 4), cmul, Op.mult, cadd, Op.add)
 
     places(slot(1), "lu", 0)
 
-    def layer(tag, xname, xa, tile, n, skip, width):
+    def layer(tag, xname, xa, to, n, skip, width):
         for b in (2, 0, 3, 1):
             mm("mw%d%s" % (b, tag), b, "w", 128 * b, xname, xa, width)
         for b in (2, 0, 3, 1):
-            out, src, nm = at(tile, b, 4 * n, 4), at("ps", 512 * b + skip, 512 * b + skip + n), "ev%d%s" % (b, tag)
+            out, src, nm = at("fil", 4 * to + b, 4 * (to + n), 4), at("ps", 512 * b + skip, 512 * b + skip + n), "ev%d%s" % (b, tag)
             if ENG.get(nm, "v" if b < 2 else "s") == "v":
                 ts(nm, out, src, 0.0, Op.max, 0.015625, Op.mult)
             else:
@@ -286,65 +291,65 @@ def rank_program(g, core, T, topo):
         NB = A - NA
         WB = max(MINC, NB)
         new = C + A * t
-        win = at("fil", 0, 4 * new)
+        win = at("fil", PRE, PRE + 4 * new)
         la_, lb_ = MINC + A * t, MINC + A * t + NA
+        ha, hb, zb, za = 0, NA, A, A + NB
         base = 2 * t
         tag = "_%d" % t
 
-        ca = NA // 4
-        cuts = list(zip(ZCUT[t][:-1], ZCUT[t][1:]))
-        for i, (c0, c1) in enumerate(cuts):
-            move("gb%d%s" % (i, tag), "s", at("opb", 16 * c0, 16 * c1), win, at("off", 48 + c0, 48 + c1))
+        def operands(r, cut, part, z, j0):
+            pb, pa = part[2] // 4, part[3] // 4
+            for i, (c0, c1) in enumerate(zip(cut[:-1], cut[1:])):
+                move("gb%s%d%s" % (r, i, tag), "s", at("opb", 4 * j0 + 16 * c0, 4 * j0 + 16 * c1), win, at("off", pb + c0, pb + c1))
+            for i, (c0, c1) in enumerate(zip(cut[:-1], cut[1:])):
+                add("ga%s%d%s" % (r, i, tag), tile(z + 4 * c0, 4 * (c1 - c0)), at("off", pa + c0, pa + c1),
+                    4 * j0 + 16 * c0, 4 * j0 + 16 * c1)
 
-        def add(i, c0, c1):
-            tile, first = ("za", 0) if c0 < ca else ("zb", ca)
-            out, offs, b = at(tile, 16 * (c0 - first), 16 * (c1 - first)), at("off", c0, c1), at("opb", 16 * c0, 16 * c1)
-            run("ga%d%s" % (i, tag), "v", lambda: g.vector.tensor_tensor(out[0], ind(win, offs), b[0], Op.add), [win, offs, b], [out])
-        for i, (c0, c1) in enumerate(cuts):
-            add(i, c0, c1)
-            if c1 == ca:
-                quant("qza" + tag, "za", MINC * t, at("za"))
-                send("sndA" + tag, t, 2 * t, "za", MINC * t, la_, NA)
-        quant("qzb" + tag, "zb", 0, at("zb", 0, 4 * WB))
+        def add(nm, out, offs, e0, e1):
+            a, b = at("opa", e0, e1), at("opb", e0, e1)
+            if nm in SPLIT.split():
+                move("gs" + nm[2:], "s", a, win, offs)
+                run(nm, "v", lambda: g.vector.tensor_tensor(out[0], a[0], b[0], Op.add), [a, b], [out])
+            else:
+                run(nm, "v", lambda: g.vector.tensor_tensor(out[0], ind(win, offs), b[0], Op.add), [win, offs, b], [out])
+
+        operands("A", ACUT[t], parts(t)[0], za, 0)
+        home = ("l", 0) if t == 0 else ("za", MINC * t)
+        quant("qza" + tag, home[0], home[1], tile(za, MINC))
+        send("sndA" + tag, t, 2 * t, home[0], home[1], la_, NA)
+        operands("B", BCUT[t], parts(t)[1], zb, NA)
+        quant("qzb" + tag, "zb", 0, tile(zb, WB))
         if t == 0:
-            unit(1)
             move("slot" + tag, "s", slot(0), slot(1))
         else:
             move("slot" + tag, "s", slot(base), slot(t - 1, 2), at("lsh", LI, LS))
-        layer("B" + tag, "zb", 0, "hb", NB, 0, WB)
-        quant("qhb" + tag, "hb", A * t, at("hb", 0, 4 * WB))
+        layer("B" + tag, "zb", 0, hb, NB, 0, WB)
+        quant("qhb" + tag, "hb", A * t, tile(hb, WB))
         send("sndB" + tag, t, 2 * t + 1, "hb", A * t, lb_, NB)
 
-        plus("cnew" + tag, "s", at("cand", 2 * A * t, 2 * A * (t + 1), 2), at("cnt", 0, A), float(new))
+        affine("cnew" + tag, "s", at("cand", 2 * A * t, 2 * A * (t + 1), 2), at("cnt", 0, A), 1.0, 4.0 * new)
         if t == 0:
             load("Lv", "y", at("vt"), T.v[:], after=[at("ql", lb_, lb_ + 1)])
-            move("sgn0", "s", at("sgn", 0, 2 * A, 2), at("zero", 0, A))
-            copy("lud", at("lu", LD, LI), at("lst", LD, LI))
-            quant("ql0", "l", 0, at("zero"))
+            ts("upick", at("lst", LU, LK), at("p16"), 127, Op.bitwise_and)
+            copy("lud", at("lu", LD, LK + 8), at("lst", LD, LK + 8))
             quant("qu", "u", 0, at("ut"))
-            ts("up0", at("upick", 0, 8), at("k8"), 16.0, Op.mult)
-            ts("up1", at("upick", 8, 16), at("zero", 0, 8), col("cf", 3), Op.add, 16.0, Op.mult)
-            ts("ids0", at("ids", 0, LS - LI), at("cnt", 0, LS - LI), 16.0, Op.mult, col("cf", 2), Op.add)
-            ts("ids1", at("ids", LS - LI), at("ids", 0, 8), 4.0, Op.mult, 3.0, Op.add)
+            ts("ids0", at("lst", LI, LS), at("lst", LK, LE), col("cf", 0), Op.add)
+            ts("ids1", at("lst", LS, LB), at("lst", LI, LI + 8), 4.0, Op.mult, 3.0, Op.add)
         move("cold" + tag, "s", at("cand", 2 * A * t + 1, 2 * A * (t + 1), 2), slot(base), at("lu", LD + 12 * t, LD + 12 * t + 12))
         if t == 0:
             run("pkq", "v", lambda: g.vector.tensor_copy(T.qp[:, 0:256].bitcast(dt.uint32),
-                                                         T.qu[:, 0:128].bitcast(dt.uint32).indirect(T.upick[:, 0:16])),
-                [at("qu"), at("upick")], [at("qp")])
-            act("pks", at("sp", 0, 256), at("su", 0, 128), Fn.Copy, offs=at("upick", 0, 16))
-            for b in (0, 2, 1, 3):
-                a = 516 * (b % 2) + 2 - 2 * (b // 2)
-                quant("qe%d" % b, "e", 128 * b, at("unit", a, a + 512))
-            ts("tie0", col("tie", 64), col("cf", 4), -2.0, Op.mult, col("cf", 3), Op.add)
-            ts("tie1", at("tie", 32, 64), at("cnt", 0, 32), 16.0, Op.is_ge, col("tie", 64), Op.subtract)
-            ts("tie2", at("tie", 0, 32), at("tie", 32, 64), -0.125, Op.mult)
-            ts("lf0", at("lf", LA + 12, LD), at("lst", LA + 12, LD), HALF + 0.25, Op.add, 1.0 / HALF, Op.mult)
-            ts("lf1", at("lf", LI, LE), at("ids"), HALF + 0.25, Op.add, 1.0 / HALF, Op.mult)
+                                                         T.qu[:, 0:128].bitcast(dt.uint32).indirect(T.lu[:, LU:LU + 16])),
+                [at("qu"), at("lu", LU, LU + 16)], [at("qp")])
+            move("pks", "s", at("sp", 0, 256), at("su", 0, 128), at("lu", LU, LU + 16))
+            for b in range(4):
+                quant("qe%d" % b, "e", 128 * b, at("unit", 3 - b, 515 - b))
+            affine("tie1", "s", at("tie", 0, 32), at("tie", 64, 96), -1.0 / 68, col("cf", 1))
+            ts("lf", at("lf", LA + 12, LD), at("lst", LA + 12, LD), HALF + 0.25, Op.add, 1.0 / HALF, Op.mult)
         if t == 1:
             move("slot3", "s", slot(3), slot(2))
             quant("qv", "v", 0, at("vt"))
         if t == 2:
-            scan("selrb", at("sel", 0, C), at("cpat"), slot(3), Op.add, Op.max)
+            scan("selrb", at("sel", 0, C), at("cpat"), slot(3))
 
         def scores(r, part, bank, j0, n, skip):
             p = 512 * bank + skip
@@ -353,48 +358,50 @@ def rank_program(g, core, T, topo):
 
         def choose(r, j0, n):
             scan("ch" + r + tag, at("nv", 2 * j0, 2 * (j0 + n)), at("sgn", 2 * j0, 2 * (j0 + n)),
-                 at("cand", 2 * (A * t + j0), 2 * (A * t + j0 + n)), Op.mult, Op.max)
+                 at("cand", 2 * (A * t + j0), 2 * (A * t + j0 + n)))
 
         def commit(r, j0, n):
             c = LD + 12 * t + j0 // 16
+            if c % 2:
+                c, j0, n = c - 1, j0 - 16, n + 16
             w, offs, in_ = slot(base), at("lu", c, c + n // 16), at("nv", 2 * j0 + 1, 2 * (j0 + n), 2)
             run("cm" + r + tag, "v", lambda: g.vector.tensor_copy(ind(w, offs), in_[0]), [in_, offs, w], [w])
 
         def unpack(r, b, q, j0, n, skip):
-            move("un%d%s%s" % (b, r, tag), q, at("fil", 4 * (new + j0) + b, 4 * (new + j0 + n), 4),
+            move("un%d%s%s" % (b, r, tag), q, at("fil", PRE + 4 * (new + j0) + b, PRE + 4 * (new + j0 + n), 4),
                  at("ps", 512 * b + skip, 512 * b + skip + n))
 
-        layer("A" + tag, "l", la_ + NA - MINC, "ha", NA, MINC - NA, MINC)
-        quant("qga" + tag, "ga", 0, at("ha"))
-        mm("moA" + tag, 4, "p", 0, "ga", 0)
+        layer("A" + tag, "l", la_ + NA - MINC, ha, NA, MINC - NA, MINC)
+        quant("qga" + tag, "ga", 0, tile(ha, MINC))
+        mm("moA" + tag, 4, "p", 128, "ga", 0)
         mm("me0A" + tag, 0, "e", 0, "ga", 0)
-        mm("mmA" + tag, 5, "p", 128, "ga", 0)
+        mm("mmA" + tag, 5, "p", 0, "ga", 0)
         for b in (2, 1, 3):
             mm("me%dA%s" % (b, tag), b, "e", 128 * b, "ga", 0)
         unpack("A", 0, "v", 0, NA, 0)
         scores("A", 0, 4, 0, NA, 0)
         choose("A", 0, NA)
-        plus("kea" + tag, "s", at("tie", 32, 64), at("tie", 0, 32), col("acc", 2))
+        affine("kea" + tag, "s", at("tie", 32, 64), at("tie", 0, 32), -4.25, col("acc", 2))
         unpack("A", 2, "s", 0, NA, 0)
         commit("A", 0, NA)
         unpack("A", 1, "s", 0, NA, 0)
         unpack("A", 3, "s", 0, NA, 0)
 
         xa, skip = lb_ + NB - WB, WB - NB
-        mm("moB" + tag, 6, "p", 0, "l", xa, WB)
-        mm("mmB" + tag, 7, "p", 128, "l", xa, WB)
+        mm("moB" + tag, 6, "p", 128, "l", xa, WB)
+        mm("mmB" + tag, 7, "p", 0, "l", xa, WB)
         for b in (0, 2, 1, 3):
             mm("me%dB%s" % (b, tag), b, "e", 128 * b, "l", xa, WB)
         scores("B", 1, 6, NA, NB, skip)
         choose("B", NA, NB)
-        plus("own" + tag, "s", col("acc", 5), col("acc", 0), col("acc", 1))
-        plus("key" + tag, "s", at("key", 0, 32), at("tie", 32, 64), col("acc", 3))
+        affine("own" + tag, "s", col("acc", 5), col("acc", 0), 1.0, col("acc", 1))
+        affine("key" + tag, "s", at("key", 0, 32), at("tie", 32, 64), 1.0, col("acc", 3))
         run("tr" + tag, "v", lambda: g.vector.transpose(T.key[:, 32:64], T.key[:, 0:32]), [at("key", 0, 32)], [at("key", 32, 64)])
         unpack("B", 0, "s", NA, NB, skip)
         commit("B", NA, NB)
         act("cmp" + tag, at("cmp"), at("key", 32, 40), Fn.Sign, scale=-1.0, bias=col("acc", 5), acc=col("acc", 6))
         side = -1.0 if t == 0 else 1.0
-        act("keep" + tag, at("keep"), col("acc", 6), Fn.Sign, scale=side, bias=4.0 * side)
+        act("keep" + tag, at("keep"), col("acc", 6), Fn.Sign, scale=side, bias=5.0 * side)
         unpack("B", 2, "s", NA, NB, skip)
         if t < ROUNDS - 1:
             a = 12 * (t + 1)
@@ -402,20 +409,19 @@ def rank_program(g, core, T, topo):
             unpack("B", 1, "v", NA, NB, skip)
             unpack("B", 3, "s", NA, NB, skip)
             places(slot(t, 2), "lsh", t + 1)
-            ts("lsi" + tag, at("lsh", LI, LS), at("lf", LI, LS), at("keep"), Op.add, HALF, Op.mult)
         else:
-            scan("selA", at("sel", C, C + T1), at("cpat", 0, T1), at("maps", 4 * C, 4 * C + T1), Op.add, Op.max)
-            ts("lsh" + tag, at("lsh", LI, LE), at("lf", LI, LE), at("keep"), Op.add, HALF, Op.mult)
+            scan("selA", at("sel", C, C + T1), at("cpat", 0, T1), at("maps", 4 * C, 4 * C + T1))
+            ts("lsh" + tag, at("lsh", LI, LB), at("lf", LI, LB), at("keep"), Op.add, HALF, Op.mult)
             unpack("B", 1, "s", NA, NB, skip)
             unpack("B", 3, "s", NA, NB, skip)
-            ts("ofA", at("off", 0, T1 // 4), at("sel", 0, C + T1), 4.0, Op.mult, col("addc", 1), Op.add, offs=at("lsh", LS, LS + T1 // 64))
-            scan("selB", at("sel", C + T1, 2 * C), at("cpat", 0, C - T1), at("maps", 4 * C + T1, 5 * C), Op.add, Op.max)
-            ts("ofB", at("off", T1 // 4), at("sel"), 4.0, Op.mult, col("addc", 1), Op.add, offs=at("lsh", LS + T1 // 64, LS + 7))
+            ts("ofT0", at("off", 0, T1 // 4), at("sel", 0, C + T1), cmul, Op.mult, cadd, Op.add, offs=at("lsh", LS, LS + T1 // 64))
+            scan("selB", at("sel", C + T1, 2 * C), at("cpat", 0, C - T1), at("maps", 4 * C + T1, 5 * C))
+            ts("ofT1", at("off", T1 // 4), at("sel"), cmul, Op.mult, cadd, Op.add, offs=at("lsh", LS + T1 // 64, LS + 7))
 
     for t in range(ROUNDS):
         one_round(t)
 
-    win = at("fil")
+    win = at("fil", PRE)
     k = 0
     for i, (c0, c1) in enumerate(zip(TG[:-1], TG[1:])):
         move("gt%d" % i, "sv"[i % 2], at("tt", 16 * c0, 16 * c1), win, at("off", c0, c1))
@@ -432,7 +438,7 @@ def rank_program(g, core, T, topo):
     for i in range(4):
         store("Ss%d" % i, "y", T.osc[4 * i:4 * i + 4, :], at("st", rows=slice(32 * i, 32 * i + 4)))
     for h in range(2):
-        move("om%d" % h, "s", at("omr", 224 * h, 224 * h + 224), slot(3, 2), at("lsh", LI + 14 * h, LI + 14 * h + 14))
+        affine("om%d" % h, "s", at("omr", 224 * h, 224 * h + 224), slot(3, 2), 0.25, -BASE / 4.0, at("lsh", LI + 14 * h, LI + 14 * h + 14))
     store("So", "y", T.om[:], at("omr", rows=slice(0, 128, 16)))
 
     for name in ([n.strip("+-") for n in ORDER.split()] or list(steps)):

from concourse.mybir import dt, AluOpType as Op, ActivationFunctionType as Fn, AxisListType as Ax

C, A, ROUNDS = 448, 192, 3
NAS = [64, 96, 96]
MINC = 128
BASE = 4096
TINY = 2.0 ** -126
HALF = C / 2
ACUT = [[0, 4, 16], [0, 6, 24], [0, 6, 24]]
BCUT = [[0, 16, 32], [0, 12, 24], [0, 12, 24]]
TCUT = [0, 128, 288, 448]
TG = [0, 20, 32, 56, 72, 96, 112]
CCUT = [0, 128, 288, 448]
YCUT = [0, 128, 288, 448]
GP = "slot3"
SPLIT = "gaB0_0 gaB1_1 gaB0_2"
T1 = 128
LANES = "co ee cc cc cc cc"
LAND = MINC + ROUNDS * A
PRE = 8 * A
F32, BF, I32, U16, Q4, U8, H16 = "float32", "bfloat16", "int32", "uint16", "float8_e4m3fn_x4", "uint8", "float16"
LM, LA, LI, LS, LB, LD, LU, LK, LE = 0, 28, 64, 92, 100, 136, 172, 180, 208
ORDER = """
La- Lm+ p16 ones Lb- Lx+ i16 Lwc- Lws+ Ld- cnt Lu- cir cia upick cf4 cib tiny c4 sgn0 cpat1+ cpat3+ cpat0+ cf chalf- cpat2- ids0 tie0 cnew_1+ unit tie1+ lum map0- map1+ lub cadd cmul lkaA_0+ lkbA_0- lkaB_0- lkbB_0+ scA_0 cnew_2+ ids1 ofA_0 scB_0 gbA1_0+ gbA0_0- ofB_0 gaA0_0 gbB1_0+ gaA1_0 gsB0_0+ qza_0 qe1 gbB0_0+ sndA_0 gaB1_0 cnew_0+ slot_0+ gaB0_0 lud qzb_0 cold_0+ lf mw1B_0 qu mw2B_0 ev1B_0+ mw3B_0 ev2B_0- mw0B_0 ev3B_0+ pks+ ev0B_0- qhb_0 qe3 sndB_0 qe0 mw3A_0 pkq mw2A_0 ev3A_0+ mw0A_0 ev2A_0- mw1A_0 ev0A_0+ ev1A_0- qga_0 qe2 moA_0 mmA_0 soA_0 Lv- chA_0 moB_0 smA_0 kea_0- cmA_0 mmB_0 soB_0 me3A_0 smB_0 chB_0 me0A_0 own_0+ key_0+ un3A_0+ tr_0 me2A_0 cmB_0 un0A_0+ cmp_0 me1A_0 un2A_0+ keep_0 me3B_0 lsh_0 me0B_0 un3B_0+ un1A_0- me2B_0 un0B_0+
lkaA_1- lkbA_1+ me1B_0 lkaB_1- lkbB_1+ scA_1 un2B_0+ ofA_1 scB_1 un1B_0+ gbA1_1+ gbA0_1- ofB_1 gaA0_1 gbB0_1+ gaA1_1 gbB1_1+ gsB1_1+ qza_1 gaB0_1 sndA_1 slot_1+ gaB1_1 qzb_1 mw0B_1 mw1B_1 ev0B_1+ mw3B_1 ev1B_1- mw2B_1 ev3B_1+ cold_1+ ev2B_1- mw0A_1 qhb_1 mw1A_1 sndB_1 slot3 ev0A_1+ mw3A_1 ev1A_1- mw2A_1 ev3A_1+ ev2A_1- qga_1 moA_1 mmA_1 soA_1 chA_1 me2A_1 smA_1 me1A_1 un2A_1+ kea_1+ me3A_1 un1A_1- cmA_1 moB_1 un3A_1+ mmB_1 soB_1 me0A_1 smB_1 chB_1 me3B_1 un0A_1+ key_1- own_1- tr_1 cmB_1 me1B_1 un3B_1+ cmp_1 me2B_1 keep_1 un1B_1+ lsh_1 me0B_1 un2B_1+
lkaA_2- lkbA_2+ lkbB_2- lkaB_2+ scA_2 un0B_1+ ofA_2 scB_2 gbA1_2+ gbA0_2- ofB_2 gaA0_2 gbB1_2+ gaA1_2 gbB0_2+ gsB0_2+ qza_2 slot_2+ gaB1_2 sndA_2 gaB0_2 qzb_2 qv mw3B_2 mw1B_2 ev3B_2+ mw2B_2 ev1B_2- mw0B_2 ev2B_2+ cold_2+ ev0B_2- mw3A_2 qhb_2 mw1A_2 sndB_2 ev3A_2+ mw2A_2 ev1A_2- mw0A_2 ev2A_2+ ev0A_2- qga_2 selrb moA_2 mmA_2 soA_2 me3A_2 smA_2 chA_2 me2A_2 un3A_2+ kea_2+ me0A_2 un2A_2- cmA_2 moB_2 un0A_2+ mmB_2 soB_2 me1A_2 smB_2 chB_2 me2B_2 un1A_2+ key_2- own_2- tr_2 cmB_2 me0B_2 un2B_2+ cmp_2 me3B_2 keep_2 un0B_2+ lsh_2 me1B_2
selA un3B_2+ ofT0 un1B_2+ selB gt0+ gt1- ofT1 qt0 gt3+ gt2- Sc0- my0 ey0+ gt4+ Sy0- qt1 gt5- my1 Sc1- ey1+ qt2 om1+ Sy1- om0- Ss0- my2 Sc2- Ss2+ ey2+ So- Ss3- Sy2+ Ss1+
"""
ENG = {n[:-1]: "s" if n[-1] == "+" else "vy"[n[0] in "SL"] for n in ORDER.split() if n[-1] in "+-"}

SCRATCH = {
    "lst": ("sbuf", [128, LE], I32), "lu": ("sbuf", [128, LE], U16),
    "lf": ("sbuf", [128, LD], F32), "lsh": ("sbuf", [128, LD], U16),
    "fil": ("sbuf", [128, PRE + 4096], BF), "maps": ("sbuf", [128, 5 * C], F32),
    "cnt": ("sbuf", [128, C], F32), "p16": ("sbuf", [128, 8], I32), "c4": ("sbuf", [128, 4], F32),
    "ci": ("sbuf", [128, 4], I32), "cf": ("sbuf", [128, 12], F32), "tiny": ("sbuf", [128, 1], F32),
    "cpat": ("sbuf", [128, C], H16), "tie": ("sbuf", [128, 96], F32),
    "ones": ("sbuf", [128, 516], BF), "unit": ("sbuf", [128, 516], BF),
    "qe": ("sbuf", [128, 512], Q4), "se": ("sbuf", [128, 512], U8),
    "qw": ("sbuf", [128, 512], Q4), "sw": ("sbuf", [128, 512], U8),
    "ut": ("sbuf", [128, 512], BF), "vt": ("sbuf", [128, 512], BF),
    "qu": ("sbuf", [128, 128], Q4), "su": ("sbuf", [128, 128], U8),
    "qp": ("sbuf", [128, 256], Q4), "sp": ("sbuf", [128, 256], U8),
    "qv": ("sbuf", [128, 128], Q4), "sv": ("sbuf", [128, 128], U8),
    "row": ("sbuf", [128, 2 * A + 32], H16), "scn": ("sbuf", [128, 2 * A + 32], H16), "off": ("sbuf", [128, 112], U16),
    "opb": ("sbuf", [128, 4 * A], BF), "opa": ("sbuf", [128, 4 * A], BF),
    "qza": ("sbuf", [128, ROUNDS * MINC], Q4), "sza": ("sbuf", [128, ROUNDS * MINC], U8),
    "qhb": ("sbuf", [128, ROUNDS * A], Q4), "shb": ("sbuf", [128, ROUNDS * A], U8),
    "qzb": ("sbuf", [128, A], Q4), "szb": ("sbuf", [128, A], U8),
    "qga": ("sbuf", [128, MINC], Q4), "sga": ("sbuf", [128, MINC], U8),
    "ql": ("sbuf", [128, LAND], Q4), "sl": ("sbuf", [128, LAND], U8),
    "sgn": ("sbuf", [128, 2 * A], BF), "cand": ("sbuf", [128, ROUNDS * 2 * A], H16), "nv": ("sbuf", [128, 2 * A], H16),
    "junk": ("sbuf", [128, A], BF), "acc": ("sbuf", [128, 8], F32), "key": ("sbuf", [128, 64], F32),
    "cmp": ("sbuf", [128, 8], F32), "keep": ("sbuf", [128, 1], F32),
    "sel": ("sbuf", [128, 2 * C], F32), "omr": ("sbuf", [128, C], F32),
    "tt": ("sbuf", [128, 4 * C], BF), "qt": ("sbuf", [128, C], Q4), "st": ("sbuf", [128, C], U8),
    "ysb": ("sbuf", [128, C], F32),
    "ps": ("psum", [128, 4096], F32),
}
SEMAPHORES = (["nv_", "ns_", "nt_", "ng_", "sent"] + ["dma%d" % k for k in range(28)]
              + ["arr%d" % k for k in range(2 * ROUNDS)])


def rank_program(g, core, T, topo):
    rank = T.rank_of(core)
    if rank is None:
        return
    queue = {"v": g.vector, "s": g.scalar, "t": g.tensor, "g": g, "y": g.sync}
    counter = {"v": "nv_", "s": "ns_", "t": "nt_", "g": "ng_"}
    known = {q: {} for q in queue}
    total, log, ndma = {}, {}, [0]
    steps = {}

    def at(name, a=0, b=None, step=1, rows=slice(None)):
        b = SCRATCH[name][1][1] if b is None else b
        if name == "ps":
            return T.ps[:, a:b], (name, 1 << (a // 512))
        bits = 0
        for c in range(a, b, step):
            bits |= 1 << c
        return (T[name][rows, a:b:step] if step > 1 else T[name][rows, a:b]), (name, bits)

    def order(q, reads, writes):
        writes = list(writes) + [r for r in reads if r[0] == "ps"]
        need = []
        for regs, w in ((reads, False), (writes, True)):
            for name, bits in regs:
                need += [e for b, e, ew in log.get(name, []) if b & bits and (w or ew)]
        for sem, n, clock, seq in sorted(need, key=lambda e: -e[3]):
            if known[q].get(sem, 0) < n:
                queue[q].wait_ge(T.sem[sem], n)
                for s, k in list(clock.items()) + [(sem, n)]:
                    known[q][s] = max(known[q].get(s, 0), k)
        return writes

    def note(reads, writes, sem, inc, clock):
        total[sem] = total.get(sem, 0) + inc
        e = (sem, total[sem], dict(clock), sum(total.values()))
        for regs, w in ((reads, False), (writes, True)):
            for name, bits in regs:
                log.setdefault(name, []).append((bits, e, w))

    def run(name, q, call, reads, writes, dma=False):
        def emit():
            r = [x[1] for x in reads]
            w = order(q, r, [x[1] for x in writes])
            if dma:
                sem, inc = "dma%d" % ndma[0], 16
                ndma[0] += 1
            else:
                sem, inc = counter[q], 1
            call().then_inc(T.sem[sem], inc)
            note(r, w, sem, inc, known[q])
        steps[name] = emit

    def ind(win, offs):
        return win[0].indirect(offs[0])

    def isap(s):
        return isinstance(s, tuple)

    def raw(s):
        return s[0] if isap(s) else s

    def copy(nm, out, in_, offs=None):
        src = ind(in_, offs) if offs else in_[0]
        run(nm, "v", lambda: g.vector.tensor_copy(out[0], src), [in_] + ([offs] if offs else []), [out])

    def ts(nm, out, in_, s1, op0, s2=None, op1=None, offs=None):
        src = ind(in_, offs) if offs else in_[0]
        reads = [in_] + [s for s in (s1, s2, offs) if isap(s)]
        if op1 is None:
            run(nm, "v", lambda: g.vector.tensor_scalar(out[0], src, raw(s1), None, op0), reads, [out])
        else:
            run(nm, "v", lambda: g.vector.tensor_scalar(out[0], src, raw(s1), raw(s2), op0, op1), reads, [out])

    def act(nm, out, in_, fn, bias=None, scale=None, acc=None, offs=None):
        src = ind(in_, offs) if offs else in_[0]
        kw = {}
        if bias is not None:
            kw["bias"] = raw(bias)
        if scale is not None:
            kw["scale"] = raw(scale)
        if acc:
            kw["accum_out"] = acc[0]
        run(nm, "s", lambda: g.scalar.activation(out[0], src, fn, **kw),
            [in_] + [s for s in (bias, scale, offs) if isap(s)], [out] + ([acc] if acc else []))

    def move(nm, q, out, in_, offs=None):
        if nm in GP.split():
            n = out[0].shape[1]
            run(nm, "g", lambda: g.affine_select(out[0], in_[0], [[0, n]], Op.is_ge, 0.0, 0, 0), [in_], [out])
        elif ENG.get(nm, q) == "v":
            copy(nm, out, in_, offs)
        else:
            act(nm, out, in_, Fn.Copy, offs=offs)

    def affine(nm, q, out, in_, scale, bias, offs=None):
        if ENG.get(nm, q) == "v":
            ts(nm, out, in_, scale, Op.mult, bias, Op.add, offs=offs)
        else:
            act(nm, out, in_, Fn.Identity, bias=bias, scale=scale, offs=offs)

    def fill(nm, out, value):
        run(nm, "v", lambda: g.vector.memset(out[0], value), [], [out])

    def scan(nm, out, d0, d1):
        run(nm, "v", lambda: g.vector.tensor_tensor_scan(out[0], d0[0], d1[0], 0.0, Op.mult, Op.max), [d0, d1], [out])

    def quant(nm, name, a, tile):
        n = tile[0].shape[1] // 4
        q, s = at("q" + name, a, a + n), at("s" + name, a, a + n)
        run(nm, "v", lambda: g.vector.quantize_mx(q[0], s[0], tile[0]), [tile], [q, s])

    def mm(nm, bank, wname, wa, xname, xa, n=MINC):
        out = at("ps", 512 * bank, 512 * bank + n)
        ops = [at("q" + wname, wa, wa + 128), at("s" + wname, wa, wa + 128),
               at("q" + xname, xa, xa + n), at("s" + xname, xa, xa + n)]
        run(nm, "t", lambda: g.tensor.matmul_mx(out[0], ops[0][0], ops[1][0], ops[2][0], ops[3][0], True, True), ops, [out])

    def load(nm, q, out, src, codes=False, after=()):
        dst = out[0].bitcast(dt.uint8) if codes else out[0]
        q = ENG.get(nm, q)
        run(nm, q, lambda: queue[q].dma_start(dst, src), list(after), [out], dma=True)

    def store(nm, q, dst, in_, codes=False):
        src = in_[0].bitcast(dt.uint8) if codes else in_[0]
        q = ENG.get(nm, q)
        run(nm, q, lambda: queue[q].dma_start(dst, src), [in_], [], dma=True)

    def iota(nm, out, pattern, base, cm, whole=False):
        kw = {} if whole else {"allow_small_or_imprecise_dtypes": True}
        run(nm, "g", lambda: g.iota(out[0], pattern, base, cm, **kw), [], [out])

    partners = [T.cores[rank ^ (1 << t)] for t in range(ROUNDS)]
    common = topo.mask(core, partners[0])
    for p in partners:
        common &= topo.mask(core, p)

    def send(nm, t, k, name, a, land, n):
        rid, pid = topo.addr(partners[t], core)
        every = topo.mask(core, partners[t])
        second = sum(1 << e for e in topo.engines(core, partners[t])[::2])
        masks = [{"c": common, "o": every & ~common, "e": every, "s": second}[c] for c in LANES.split()[k]]
        lanes = sum(bin(m).count("1") for m in masks)
        sem = "arr%d" % k
        src = [at("q" + name, a, a + n), at("s" + name, a, a + n)]
        dst = [at("ql", land, land + n), at("sl", land, land + n)]

        def emit():
            order("g", [s[1] for s in src], [])
            g.remote_dma(dst[0][0].bitcast(dt.uint8), src[0][0].bitcast(dt.uint8), T.sem[sem], T.sem.sent, pid, rid, masks[0])
            g.remote_dma(dst[1][0], src[1][0], T.sem[sem], T.sem.sent, pid, rid, masks[1])
            total["sent"] = total.get("sent", 0) + lanes
            note([], [d[1] for d in dst], sem, lanes, {})
        steps[nm] = emit

    def slot(k, n=1):
        return at("maps", C * k, C * (k + n))

    def col(name, k):
        return at(name, k, k + 1)

    def tile(a, n):
        return at("fil", 4 * a, 4 * (a + n))

    load("Lm", "y", at("lst", LM, LA), T.m[:])
    load("La", "s", at("lst", LA, LI), T.la[:])
    load("Lb", "y", at("lst", LB, LD), T.lb[:])
    load("Lx", "y", at("fil", PRE, PRE + 4 * C), T.x[:])
    load("Lwc", "y", at("qw"), T.wc[:], codes=True)
    load("Lws", "y", at("sw"), T.ws[:])
    load("Ld", "y", at("lst", LD, LU), T.ld[:])
    load("Lu", "y", at("ut"), T.u[:])

    iota("p16", at("p16"), [[0, 8]], 0, 16, whole=True)
    iota("cnt", at("cnt"), [[4, C]], BASE, 0)
    iota("i16", at("lst", LK, LE), [[16, LE - LK]], 0, 0, whole=True)
    iota("tie0", at("tie", 64, 96), [[-2, 2], [0, 16]], 1, 2)
    fill("tiny", at("tiny"), TINY)
    fill("ones", at("ones"), 1.0)
    fill("sgn0", at("sgn"), 0.0)
    ts("cir", col("ci", 0), col("p16", 0), 255, Op.bitwise_and, 4, Op.logical_shift_right)
    ts("cia", col("ci", 1), col("p16", 0), 9, Op.logical_shift_right)
    ts("cib", col("ci", 2), col("p16", 0), 63, Op.bitwise_and, 4, Op.logical_shift_right)
    copy("cf", at("cf", 0, 2), at("ci", 0, 2))
    ts("cf4", col("cf", 8), col("ci", 0), 4.0, Op.mult)
    ts("cadd", col("cf", 2), col("ci", 2), -float(BASE), Op.add)
    ts("c4", at("c4"), at("lst", LK, LK + 4), col("cf", 8), Op.is_gt, 2.0, Op.mult)
    for k in range(4):
        affine("cpat%d" % k, "s", at("cpat", k, C, 4), at("ones", 0, C // 4), col("c4", k), 0.0)
    affine("chalf", "v", at("cf", 4, 8), at("c4"), -0.25, 1.0)
    run("cmul", "v", lambda: g.vector.tensor_reduce(T.cf[:, 3:4], T.cf[:, 4:8], Ax.X, Op.mult), [at("cf", 4, 8)], [col("cf", 3)])
    cmul, cadd = col("cf", 3), col("cf", 2)
    run("unit", "g", lambda: g.affine_select(T.unit[:], T.ones[:], [[-1, 516]], Op.is_equal, 0.0, 3, 4), [at("ones")], [at("unit")])

    copy("lum", at("lu", LM, LA + 12), at("lst", LM, LA + 12))
    move("map0", "v", at("maps", C, C + 224), at("cnt"), at("lu", LM, LM + 14))
    move("map1", "s", at("maps", C + 224, 2 * C), at("cnt"), at("lu", LM + 14, LA))
    copy("lub", at("lu", LB, LB + 12), at("lst", LB, LB + 12))

    def parts(t):
        na = NAS[t] // 16
        gap = 16 * (na % 2)
        b2 = 32 * na + gap
        return [(0, na, 0, 16 * na, 0), (na - na % 2, 12 - na + na % 2, b2, b2 + A - 16 * na + gap, gap)]

    def places(win, lists, t):
        for r, (c0, n, pb, pa, gap) in zip("AB", parts(t)):
            for o, l, p in (("b", LB, pb), ("a", LA, pa)):
                move("lk%s%s_%d" % (o, r, t), "v" if (o, r) == ("a", "A") else "s", at("row", p - gap, p - gap + 16 * n), win,
                     at(lists, l + 12 * t + c0, l + 12 * t + c0 + n))
            end = pa - gap + 16 * n
            scan("sc%s_%d" % (r, t), at("scn", pb, end), at("cpat", 0, end - pb), at("row", pb, end))
            ts("of%s_%d" % (r, t), at("off", pb // 4, end // 4), at("scn", pb + 3, end, 4), cmul, Op.mult, cadd, Op.add)

    places(slot(1), "lu", 0)

    def layer(tag, xname, xa, to, n, skip, width):
        for b in (2, 0, 3, 1):
            mm("mw%d%s" % (b, tag), b, "w", 128 * b, xname, xa, width)
        for b in (2, 0, 3, 1):
            out, src, nm = at("fil", 4 * to + b, 4 * (to + n), 4), at("ps", 512 * b + skip, 512 * b + skip + n), "ev%d%s" % (b, tag)
            if ENG.get(nm, "v" if b < 2 else "s") == "v":
                ts(nm, out, src, 0.0, Op.max, 0.015625, Op.mult)
            else:
                act(nm, out, src, Fn.Relu, scale=0.015625)

    def one_round(t):
        NA = NAS[t]
        NB = A - NA
        WB = max(MINC, NB)
        new = C + A * t
        win = at("fil", PRE, PRE + 4 * new)
        la_, lb_ = MINC + A * t, MINC + A * t + NA
        ha, hb, zb, za = 0, NA, A, A + NB
        base = 2 * t
        tag = "_%d" % t

        def operands(r, cut, part, z, j0):
            pb, pa = part[2] // 4, part[3] // 4
            for i, (c0, c1) in enumerate(zip(cut[:-1], cut[1:])):
                move("gb%s%d%s" % (r, i, tag), "s", at("opb", 4 * j0 + 16 * c0, 4 * j0 + 16 * c1), win, at("off", pb + c0, pb + c1))
            for i, (c0, c1) in enumerate(zip(cut[:-1], cut[1:])):
                add("ga%s%d%s" % (r, i, tag), tile(z + 4 * c0, 4 * (c1 - c0)), at("off", pa + c0, pa + c1),
                    4 * j0 + 16 * c0, 4 * j0 + 16 * c1)

        def add(nm, out, offs, e0, e1):
            a, b = at("opa", e0, e1), at("opb", e0, e1)
            if nm in SPLIT.split():
                move("gs" + nm[2:], "s", a, win, offs)
                run(nm, "v", lambda: g.vector.tensor_tensor(out[0], a[0], b[0], Op.add), [a, b], [out])
            else:
                run(nm, "v", lambda: g.vector.tensor_tensor(out[0], ind(win, offs), b[0], Op.add), [win, offs, b], [out])

        operands("A", ACUT[t], parts(t)[0], za, 0)
        home = ("l", 0) if t == 0 else ("za", MINC * t)
        quant("qza" + tag, home[0], home[1], tile(za, MINC))
        send("sndA" + tag, t, 2 * t, home[0], home[1], la_, NA)
        operands("B", BCUT[t], parts(t)[1], zb, NA)
        quant("qzb" + tag, "zb", 0, tile(zb, WB))
        if t == 0:
            move("slot" + tag, "s", slot(0), slot(1))
        else:
            move("slot" + tag, "s", slot(base), slot(t - 1, 2), at("lsh", LI, LS))
        layer("B" + tag, "zb", 0, hb, NB, 0, WB)
        quant("qhb" + tag, "hb", A * t, tile(hb, WB))
        send("sndB" + tag, t, 2 * t + 1, "hb", A * t, lb_, NB)

        affine("cnew" + tag, "s", at("cand", 2 * A * t, 2 * A * (t + 1), 2), at("cnt", 0, A), 1.0, 4.0 * new)
        if t == 0:
            load("Lv", "y", at("vt"), T.v[:], after=[at("ql", lb_, lb_ + 1)])
            ts("upick", at("lst", LU, LK), at("p16"), 127, Op.bitwise_and)
            copy("lud", at("lu", LD, LK + 8), at("lst", LD, LK + 8))
            quant("qu", "u", 0, at("ut"))
            ts("ids0", at("lst", LI, LS), at("lst", LK, LE), col("cf", 0), Op.add)
            ts("ids1", at("lst", LS, LB), at("lst", LI, LI + 8), 4.0, Op.mult, 3.0, Op.add)
        move("cold" + tag, "s", at("cand", 2 * A * t + 1, 2 * A * (t + 1), 2), slot(base), at("lu", LD + 12 * t, LD + 12 * t + 12))
        if t == 0:
            run("pkq", "v", lambda: g.vector.tensor_copy(T.qp[:, 0:256].bitcast(dt.uint32),
                                                         T.qu[:, 0:128].bitcast(dt.uint32).indirect(T.lu[:, LU:LU + 16])),
                [at("qu"), at("lu", LU, LU + 16)], [at("qp")])
            move("pks", "s", at("sp", 0, 256), at("su", 0, 128), at("lu", LU, LU + 16))
            for b in range(4):
                quant("qe%d" % b, "e", 128 * b, at("unit", 3 - b, 515 - b))
            affine("tie1", "s", at("tie", 0, 32), at("tie", 64, 96), -1.0 / 68, col("cf", 1))
            ts("lf", at("lf", LA + 12, LD), at("lst", LA + 12, LD), HALF + 0.25, Op.add, 1.0 / HALF, Op.mult)
        if t == 1:
            move("slot3", "s", slot(3), slot(2))
            quant("qv", "v", 0, at("vt"))
        if t == 2:
            scan("selrb", at("sel", 0, C), at("cpat"), slot(3))

        def scores(r, part, bank, j0, n, skip):
            p = 512 * bank + skip
            act("so" + r + tag, at("sgn", 2 * j0 + 1, 2 * (j0 + n), 2), at("ps", p, p + n), Fn.Sign, bias=at("tiny"), acc=col("acc", part))
            act("sm" + r + tag, at("junk", j0, j0 + n), at("ps", p + 512, p + 512 + n), Fn.Sign, bias=at("tiny"), acc=col("acc", 2 + part))

        def choose(r, j0, n):
            scan("ch" + r + tag, at("nv", 2 * j0, 2 * (j0 + n)), at("sgn", 2 * j0, 2 * (j0 + n)),
                 at("cand", 2 * (A * t + j0), 2 * (A * t + j0 + n)))

        def commit(r, j0, n):
            c = LD + 12 * t + j0 // 16
            if c % 2:
                c, j0, n = c - 1, j0 - 16, n + 16
            w, offs, in_ = slot(base), at("lu", c, c + n // 16), at("nv", 2 * j0 + 1, 2 * (j0 + n), 2)
            run("cm" + r + tag, "v", lambda: g.vector.tensor_copy(ind(w, offs), in_[0]), [in_, offs, w], [w])

        def unpack(r, b, q, j0, n, skip):
            move("un%d%s%s" % (b, r, tag), q, at("fil", PRE + 4 * (new + j0) + b, PRE + 4 * (new + j0 + n), 4),
                 at("ps", 512 * b + skip, 512 * b + skip + n))

        layer("A" + tag, "l", la_ + NA - MINC, ha, NA, MINC - NA, MINC)
        quant("qga" + tag, "ga", 0, tile(ha, MINC))
        mm("moA" + tag, 4, "p", 128, "ga", 0)
        mm("me0A" + tag, 0, "e", 0, "ga", 0)
        mm("mmA" + tag, 5, "p", 0, "ga", 0)
        for b in (2, 1, 3):
            mm("me%dA%s" % (b, tag), b, "e", 128 * b, "ga", 0)
        unpack("A", 0, "v", 0, NA, 0)
        scores("A", 0, 4, 0, NA, 0)
        choose("A", 0, NA)
        affine("kea" + tag, "s", at("tie", 32, 64), at("tie", 0, 32), -4.25, col("acc", 2))
        unpack("A", 2, "s", 0, NA, 0)
        commit("A", 0, NA)
        unpack("A", 1, "s", 0, NA, 0)
        unpack("A", 3, "s", 0, NA, 0)

        xa, skip = lb_ + NB - WB, WB - NB
        mm("moB" + tag, 6, "p", 128, "l", xa, WB)
        mm("mmB" + tag, 7, "p", 0, "l", xa, WB)
        for b in (0, 2, 1, 3):
            mm("me%dB%s" % (b, tag), b, "e", 128 * b, "l", xa, WB)
        scores("B", 1, 6, NA, NB, skip)
        choose("B", NA, NB)
        affine("own" + tag, "s", col("acc", 5), col("acc", 0), 1.0, col("acc", 1))
        affine("key" + tag, "s", at("key", 0, 32), at("tie", 32, 64), 1.0, col("acc", 3))
        run("tr" + tag, "v", lambda: g.vector.transpose(T.key[:, 32:64], T.key[:, 0:32]), [at("key", 0, 32)], [at("key", 32, 64)])
        unpack("B", 0, "s", NA, NB, skip)
        commit("B", NA, NB)
        act("cmp" + tag, at("cmp"), at("key", 32, 40), Fn.Sign, scale=-1.0, bias=col("acc", 5), acc=col("acc", 6))
        side = -1.0 if t == 0 else 1.0
        act("keep" + tag, at("keep"), col("acc", 6), Fn.Sign, scale=side, bias=5.0 * side)
        unpack("B", 2, "s", NA, NB, skip)
        if t < ROUNDS - 1:
            a = 12 * (t + 1)
            ts("lsh" + tag, at("lsh", LA + a, LB + a + 12), at("lf", LA + a, LB + a + 12), at("keep"), Op.add, HALF, Op.mult)
            unpack("B", 1, "v", NA, NB, skip)
            unpack("B", 3, "s", NA, NB, skip)
            places(slot(t, 2), "lsh", t + 1)
        else:
            scan("selA", at("sel", C, C + T1), at("cpat", 0, T1), at("maps", 4 * C, 4 * C + T1))
            ts("lsh" + tag, at("lsh", LI, LB), at("lf", LI, LB), at("keep"), Op.add, HALF, Op.mult)
            unpack("B", 1, "s", NA, NB, skip)
            unpack("B", 3, "s", NA, NB, skip)
            ts("ofT0", at("off", 0, T1 // 4), at("sel", 0, C + T1), cmul, Op.mult, cadd, Op.add, offs=at("lsh", LS, LS + T1 // 64))
            scan("selB", at("sel", C + T1, 2 * C), at("cpat", 0, C - T1), at("maps", 4 * C + T1, 5 * C))
            ts("ofT1", at("off", T1 // 4), at("sel"), cmul, Op.mult, cadd, Op.add, offs=at("lsh", LS + T1 // 64, LS + 7))

    for t in range(ROUNDS):
        one_round(t)

    win = at("fil", PRE)
    k = 0
    for i, (c0, c1) in enumerate(zip(TG[:-1], TG[1:])):
        move("gt%d" % i, "sv"[i % 2], at("tt", 16 * c0, 16 * c1), win, at("off", c0, c1))
        if 4 * c1 == TCUT[k + 1]:
            a, b = TCUT[k], TCUT[k + 1]
            quant("qt%d" % k, "t", a, at("tt", 4 * a, 4 * b))
            mm("my%d" % k, k, "v", 0, "t", a, b - a)
            move("ey%d" % k, "s", at("ysb", a, b), at("ps", 512 * k, 512 * k + b - a))
            k += 1
    for k, (a, b) in enumerate(zip(CCUT[:-1], CCUT[1:])):
        store("Sc%d" % k, "y", T.oc[:, 4 * a:4 * b], at("qt", a, b), codes=True)
    for k, (a, b) in enumerate(zip(YCUT[:-1], YCUT[1:])):
        store("Sy%d" % k, "y", T.y[:, a:b], at("ysb", a, b))
    for i in range(4):
        store("Ss%d" % i, "y", T.osc[4 * i:4 * i + 4, :], at("st", rows=slice(32 * i, 32 * i + 4)))
    for h in range(2):
        affine("om%d" % h, "s", at("omr", 224 * h, 224 * h + 224), slot(3, 2), 0.25, -BASE / 4.0, at("lsh", LI + 14 * h, LI + 14 * h + 14))
    store("So", "y", T.om[:], at("omr", rows=slice(0, 128, 16)))

    for name in ([n.strip("+-") for n in ORDER.split()] or list(steps)):
        steps[name]()
    for sem, n in total.items():
        g.wait_ge(T.sem[sem], n)
